import numpy as np, ml_dtypes
CORES = [16,18,20,22]
N = 4
BF = ml_dtypes.bfloat16
def gentries(a):
    return np.ascontiguousarray(a.reshape(8, 16, -1).transpose(0, 2, 1)).reshape(8, -1)
def gtable(e):
    e = np.asarray(e); return np.ascontiguousarray(e.reshape(8, -1, 16).transpose(0, 2, 1)).reshape(128, -1).astype(np.int32)
V, H, RO, SQ, K = 3072, 256, 3, 4, 128
W = V + 2 * H; Z = 8 * N
def ring(a):
    return np.ascontiguousarray(np.swapaxes(a, 0, 1)).reshape((Z,) + a.shape[2:])
def unring(a):
    return np.ascontiguousarray(np.swapaxes(a.reshape((8, N) + a.shape[1:]), 0, 1))
def tiles(a):
    return np.ascontiguousarray(unring(a).transpose(0, 1, 3, 2)).reshape(N, 128, V)
def pack(x, lf, rt):
    return {"x0": (tiles(x).astype(np.float32) * np.float32(0.015625)).astype(BF), "lf": np.stack([gtable(a) for a in unring(lf)]), "rt": np.stack([gtable(a) for a in unring(rt)])}
def loose(rng):
    v = np.arange(H, H + V)
    return (rng.random((Z, V)) * v).astype(np.int64), v + 1 + (rng.random((Z, V)) * (W - 1 - v)).astype(np.int64)
def textures(rng, lf, rt, scale):
    B = V // 4; i = np.arange(4)
    prof = (rng.integers(0, 257, (K, 4, 16)) * scale).astype(np.int64); good = rng.integers(0, 5, K); amp = rng.choice(np.array([2, 8, 20, 40]), (K, 1, 1))
    lab = np.minimum((K * rng.random((Z, B)) ** 2).astype(np.int64), K - 1)
    x = prof[lab] + np.rint((2 * rng.random((Z, B, 4, 16)) - 1) * amp[lab]).astype(np.int64)
    for z in range(Z):
        o = np.argsort(lab[z], kind="stable"); a, b = o[:-1], o[1:]; s = lab[z][a] == lab[z][b]; a, b = a[s], b[s]
        g = good[lab[z][a]][:, None]; on = (g == i) | (g == 4); u = rng.random((a.size, 1))
        pa = 4 * a[:, None] + i; pb = 4 * b[:, None] + i
        m = on & (u > 0.04); rt[z, pa[m]] = H + pb[m]
        m = on & (u < 0.96); lf[z, pb[m]] = H + pa[m]
        y = (z + 1) % Z
        last = np.full(K, -1); last[lab[z]] = np.arange(B); first = np.full(K, B); first[lab[y][::-1]] = np.arange(B)[::-1]
        k = np.nonzero((last >= (V - H) // 4) & (first < H // 4))[0]
        g = good[k][:, None]; on = (g == i) | (g == 4); pa = 4 * last[k][:, None] + i; pb = 4 * first[k][:, None] + i
        rt[z, pa[on]] = H + V + pb[on]; lf[y, pb[on]] = H - V + pa[on]
    return np.clip(x, 0, 256).reshape(Z, V, 16)
def setup_inputs(rng):
    lf, rt = loose(rng); x = textures(rng, lf, rt, 1)
    return pack(x, lf, rt)
def setup_inputs_spread(rng):
    v = np.arange(H, H + V)
    lf = v - np.floor(np.power(1.0 * v, rng.random((Z, V)))).astype(np.int64)
    rt = v + np.floor(np.power(1.0 * (W - 1 - v), rng.random((Z, V)))).astype(np.int64)
    x = textures(rng, lf, rt, rng.choice(np.array([1.0, 0.5, 0.25]), (K, 1, 16), p=[0.5, 0.25, 0.25]))
    return pack(x * (rng.random((Z, V, 1)) > 0.03), lf, rt)
def setup_inputs_ends(rng):
    v = np.arange(H, H + V); near = np.zeros((Z, V), bool); n = V // 2 + 40
    for z in range(Z):
        runs = np.stack([rng.integers(1, 21, n), rng.integers(1, 51, n)], axis=1).reshape(-1); o = rng.integers(0, 40)
        near[z] = np.repeat(np.arange(2 * n) % 2 == 0, runs)[o:o + V]
        g = z // N
        if g % 2 == 0 or g == 7: near[z, 0] = True
        if g % 2 == 1: near[z, V - 1] = True
    near[Z - 1, V - 30:] = True
    arch = rng.integers(0, 2, 16); flip = rng.random((Z, V, 16)) < rng.choice(np.array([0.0, 0.1, 0.4]), (Z, V, 1))
    x = 256 * ((arch + rng.integers(0, 2, (Z, V, 1)) + flip) % 2)
    x = np.where(rng.random((Z, V, 1)) < 0.28, rng.integers(0, 257, (Z, V, 16)), x)
    return pack(x, np.where(near, v - 1, 0), np.where(near, v + 1, W - 1))
def setup_inputs_corners(rng):
    lf, rt = loose(rng); x = np.zeros((Z, V, 16), np.int64); T = 2 ** SQ
    sizes = [[1], [1, 2, 3], [3, 4, 5], [T - 1, T, T + 1, T + 2], [3 * T], [V], [1, 2, 3, 4, T, T + 1, 2 * T], [4]]
    for z in range(Z):
        k = np.array(sizes[(z // N + z % N) % 8]); n = rng.choice(k, V // int(k.min()) + 1)
        lab = np.empty(V, np.int64); lab[rng.permutation(V)] = np.repeat(np.arange(n.size), n)[:V]
        o = np.argsort(lab, kind="stable"); a, b = o[:-1], o[1:]; s = lab[a] == lab[b]; a, b = a[s], b[s]
        rt[z, a] = H + b; lf[z, b] = H + a
        amp = 40 if k[0] == V else 3
        x[z] = rng.integers(0, 257, (V, 16))[lab] + rng.integers(-amp, amp + 1, (V, 16))
    for z in range(Z):
        y = (z + 1) % Z
        if (z // N) % 2 == 0: rt[z, V - 1] = H + V; lf[y, 0] = H - 1
        else: rt[z, V - H] = W - 1; lf[y, H - 1] = 0
    return pack(np.clip(x, 0, 256), lf, rt)
def setup_inputs_crowd(rng):
    lf, rt = loose(rng); x = textures(rng, lf, rt, 1); v = np.arange(H, H + V); kind = rng.permutation(8)
    for z in range(Z):
        k = kind[z // N]
        if k < 2:
            j = rng.integers(0, V); a, b = lf[z, j], rt[z, j]; lf[z] = 0; rt[z] = W - 1
            if k == 1: lf[z, j] = a; rt[z, j] = b
        elif k == 2:
            rt[z] = np.where(v < H + V - 1, H + V - 1, W - 1); lf[z] = np.where(v > H, H, 0)
        elif k == 3:
            h = np.sort(H + rng.permutation(V)[:5])
            rt[z] = np.concatenate([h, [W - 1]])[np.searchsorted(h, v, side="right")]
            lf[z] = np.concatenate([[0], h])[np.searchsorted(h, v, side="left")]
    return pack(x, lf, rt)
def setup_inputs_calm(rng):
    lf, rt = loose(rng); x = textures(rng, lf, rt, 1); kind = rng.permutation(8)
    for z in range(Z):
        k = kind[z // N] % 4
        if k < 3: x[z] = (0, 253, 192)[k] + rng.integers(0, 4, (V, 16))
    return pack(x, lf, rt)
def check_ranges(d):
    bad = []; v = np.arange(H, H + V)
    x = np.asarray(d["x0"]).astype(np.float64)
    if not np.all((x >= 0) & (x <= 4)): bad.append("range of x0")
    elif np.any(x * 64 != np.floor(x * 64)): bad.append("x0 holds a number that is no multiple of 2**-6")
    elif np.min(np.mean(x.reshape(N, -1), axis=1)) < 1: bad.append("the mean of a rank's x0 is under 1")
    a = np.stack([gentries(e) for e in np.asarray(d["lf"])]).astype(np.int64); b = np.stack([gentries(e) for e in np.asarray(d["rt"])]).astype(np.int64)
    if np.min(a) < 0 or np.max(a) > H + V - 2: bad.append("range of lf")
    if np.any(a >= v): bad.append("an entry of lf isn't under its place")
    if np.min(b) < H + 1 or np.max(b) > W - 1: bad.append("range of rt")
    if np.any(b <= v): bad.append("an entry of rt isn't over its place")
    return bad
def pick(w, i):
    return w.reshape(-1, 16)[i + w.shape[1] * np.arange(Z)[:, None]]
def better(w, x, c, cur):
    c = np.where((c >= 0) & (c < W), c, cur)
    near = np.abs(pick(w, c) - x) < np.abs(pick(w, cur) - x)
    return np.where(np.add.reduce(near.astype(np.int64), axis=2) >= 9, c, cur)
def reference(x0, lf, rt):
    x = ring(np.asarray(x0).astype(np.float32).reshape(N, 8, 16, V).transpose(0, 1, 3, 2))
    l = ring(np.stack([gentries(a) for a in lf]).astype(np.int64)); r = ring(np.stack([gentries(a) for a in rt]).astype(np.int64))
    y = np.zeros((Z, V, 16)); own = np.arange(H, H + V)
    for t in range(RO):
        w = np.concatenate([np.roll(x, 1, axis=0)[:, V - H:], x, np.roll(x, -1, axis=0)[:, :H]], axis=1)
        if t % 2 == 0:
            cl = np.concatenate([np.roll(l, 1, axis=0)[:, V - 1:] - V, l[:, :V - 1]], axis=1) + 1
            cr = np.concatenate([np.roll(r, 1, axis=0)[:, V - 1:] - V, r[:, :V - 1]], axis=1) + 1
        else:
            cl = np.concatenate([l[:, 1:], np.roll(l, -1, axis=0)[:, :1] + V], axis=1) - 1
            cr = np.concatenate([r[:, 1:], np.roll(r, -1, axis=0)[:, :1] + V], axis=1) - 1
        l = better(w, x, cl, l); r = better(w, x, cr, r)
        rw = np.concatenate([np.roll(r, 1, axis=0)[:, V - H:] - V, r], axis=1)
        lw = np.concatenate([l, np.roll(l, -1, axis=0)[:, :H] + V], axis=1)
        back = np.where(np.take_along_axis(rw, l, 1) == own, l, own)
        end = np.take_along_axis(lw, r - H, 1) != own
        a = np.concatenate([np.tile(np.arange(H), (Z, 1)), back], axis=1); n = (a != np.arange(H + V)).astype(np.int64); m = np.ascontiguousarray(w[:, :H + V])
        for k in range(SQ):
            m = np.maximum(m, pick(m, a)); n = n + np.take_along_axis(n, a, 1); a = np.take_along_axis(a, a, 1)
        y = y + m[:, H:].astype(np.float64) * np.exp(-np.abs(x - pick(w, r)).astype(np.float64))
        go = end & (n[:, H:] >= 3)
        moved = np.minimum(np.maximum(x + np.float32(0.125) * (x - pick(w, a[:, H:])), np.float32(0)), np.float32(4))
        x = np.where(go[:, :, None], moved, x)
    return {"xe": tiles(x).astype(np.float32), "ye": tiles(y).astype(np.float32)}

def check_inputs(d):
    bad = list(check_ranges(d))
    if not bad:
        for name, y in reference(**d).items():
            for q in range(N):
                v = np.abs(np.asarray(y[q], np.float64)); s = np.sqrt(np.mean(v * v))
                if v.max() > 5 * s or s < 2.0 ** -1: bad.append('%s of rank %d is uneven or too small' % (name, q))
    return bad

@@ -1,0 +1,822 @@
+from concourse.bass import DstId, RemoteDMATransfer
+from concourse.mybir import dt, AluOpType, AxisListType, ActivationFunctionType
+
+A = AluOpType
+F = ActivationFunctionType
+V, H, RO = 3072, 256, 3
+PAD = 64
+O0 = PAD + H
+O1 = O0 + V
+WP = O1 + H + PAD
+C0, C1, CW = O0 // 16, O1 // 16, WP // 16
+K = V // 16
+FAR = 16.0
+
+KD = "BHF"
+OPT = {
+    "form": ["ssssss", "ssssss", "acacac"],
+    "w": ["svs", "svs", "svs"],
+    "rl": ["svs", "svs", "svs"], "lr": ["sss", "sss", "sss"],
+    "a2": ["sss", "sss", "sss"], "a4": ["sss", "sss", "sss"], "a8": ["sss", "sss", "sss"],
+    "x8": ["sss", "sss", "sss"], "xs": ["sssss", "sssss", "sssss"],
+    "hi": ["sss", "sss", "sss"],
+}
+PARTS = [2, 2, 2]
+LOPE = (1, 1, 0)
+GROUPS = {("R", 2): (128, 192), ("R", 1): (0, 128), ("L", 1): (0, 128), ("L", 2): (128, 192)}
+SLACK, PASSES, TRIES, TEMP, SEED, ALT = (0.8,), 3, 70000, 0.6, 1, [(0.85, 1.7)]
+
+f32, b16, f16, i32, u16 = "float32", "bfloat16", "float16", "int32", "uint16"
+US = ["eR", "eL", "cR", "cL", "tR", "tL", "a1", "ta", "a2", "a4", "a8", "s"]
+MF = ["I", "nI", "S1p", "S2p", "S1m", "S2m", "I232", "RL", "RR", "P9", "N1", "I2", "nI2"]
+MB = ["I", "nI", "I2", "nI2", "P9", "N1", "P9L", "N1L", "P9R", "N1R", "I3712", "I7"]
+MH = ["I", "nI3712", "nI", "I2", "nI2", "P9", "N1", "P9L", "N1L", "P9R", "N1R"]
+HALF = True
+ENG = {"s": "scalar", "v": "vector"}
+
+SCRATCH = {
+    "XB": ("sbuf", [128, WP + O1], b16),
+    "XF": ("sbuf", [128, 2 * WP + O1], f32),
+    "MA": ("sbuf", [128, O1], f32), "MB": ("sbuf", [128, O1], f32),
+    "TR": ("sbuf", [128, WP], b16), "TL": ("sbuf", [128, WP], b16),
+    "A2": ("sbuf", [128, O1], b16), "A4": ("sbuf", [128, O1], b16),
+    "FA": ("sbuf", [128, 2048], f32), "FB": ("sbuf", [128, 2048], f32),
+    "DW": ("sbuf", [128, V], f32), "MP": ("sbuf", [128, V], f32),
+    "GE": ("sbuf", [128, V], b16), "PP": ("sbuf", [128, V], b16),
+    "NE": ("sbuf", [128, V], b16),
+    "VI": ("sbuf", [128, 2048], b16),
+    "U": ("sbuf", [128, K * len(US)], u16),
+    "NR": ("sbuf", [128, 4 * CW], f32), "NL": ("sbuf", [128, 4 * CW], f32),
+    "HR": ("sbuf", [128, 2 * CW], b16), "HL": ("sbuf", [128, 2 * CW], b16), "HA": ("sbuf", [128, 2 * CW], b16),
+    "NA": ("sbuf", [128, K], f32), "TT": ("sbuf", [128, 2 * K], f32), "QM": ("sbuf", [128, 3 * K], f16),
+    "EN": ("sbuf", [128, K], f32), "HH": ("sbuf", [128, K], f32), "GO": ("sbuf", [128, K], f32),
+    "IO": ("sbuf", [128, CW], f32), "ONF": ("sbuf", [128, K], f32), "ONB": ("sbuf", [128, K], b16),
+    "LI": ("sbuf", [128, 2 * K], i32), "SI": ("sbuf", [128, 128], i32), "GI": ("sbuf", [128, 128], i32),
+    "SXB": ("sbuf", [128, 512], b16), "SXF": ("sbuf", [128, 1024], f32), "SE": ("sbuf", [128, 6 * 32], f32),
+    "MTF": ("sbuf", [128, 128 * len(MF)], f32), "MTB": ("sbuf", [128, 128 * len(MB)], b16),
+    "MTH": ("sbuf", [128, 128 * (len(MH) if HALF else 2)], f16),
+    "KI": ("sbuf", [128, 8], i32), "KF": ("sbuf", [128, 8], f32), "RW": ("sbuf", [128, O0], f32),
+    "QA": ("psum", [128, 1024], f32), "QB": ("psum", [128, 1024], f32),
+    "E0": ("psum", [128, 512], f32), "E1": ("psum", [128, 512], f32),
+    "LA": ("psum", [128, 512], f32), "LB": ("psum", [128, 512], f32),
+}
+if HALF:
+    SCRATCH["GH"] = ("sbuf", [128, V], f16)
+    SCRATCH["PH"] = ("sbuf", [128, V], f16)
+    SCRATCH["XH"] = ("sbuf", [128, V], f16)
+PSUM = ("QA", "QB", "E0", "E1", "LA", "LB")
+NDMA = 100
+SEMAPHORES = ["vector", "scalar", "tensor", "gcomp", "sent"] + ["arr%d" % k for k in range(12)] + ["d%d" % k for k in range(NDMA)]
+
+CY, GA, PC, HOP = 0.00083 * 1.25, 1.56, 0.00042 * 1.25, 0.1
+
+
+def build(g, core, T, topo):
+    rank = T.rank_of(core)
+    n = len(T.cores)
+    left, right = T.cores[(rank - 1) % n], T.cores[(rank + 1) % n]
+    turn_l, turn_r = rank == 0, rank == n - 1
+    ops = []
+    vq, sq, pq = g.vector, g.scalar, g.tensor
+
+    def ap(r):
+        return T[r[0]][:, r[1]:r[2]]
+
+    def add(eng, fn, r, w, cost, lat=0.0, kind="c", cnt=1):
+        ops.append(dict(eng=eng, fn=fn, r=list(r), w=list(w), cost=cost, lat=lat, kind=kind, cnt=cnt))
+        return len(ops) - 1
+
+    def two(r):
+        return SCRATCH[r[0]][2] in (b16, f16, u16)
+
+    def vc(nel, f):
+        return 0.06 + max(64, nel * f) * CY
+
+    def ts(o, i, s1, s2, o0, o1=None, extra=()):
+        f = 0.5 if two(o) and two(i) else 1.0
+        if o1 is None:
+            fn = lambda: vq.tensor_scalar(ap(o), ap(i), s1, None, o0)
+        else:
+            fn = lambda: vq.tensor_scalar(ap(o), ap(i), s1, s2, o0, o1)
+        return add("vector", fn, [i] + list(extra), [o], vc(o[2] - o[1], f))
+
+    def cp(o, i):
+        f = 0.5 if two(o) and two(i) else 1.0
+        return add("vector", lambda: vq.tensor_copy(ap(o), ap(i)), [i], [o], vc(o[2] - o[1], f))
+
+    def tt(o, a, b, op):
+        f = 1.0 if a[0] in PSUM or b[0] in PSUM else 2.0
+        return add("vector", lambda: vq.tensor_tensor(ap(o), ap(a), ap(b), op), [a, b], [o], vc(o[2] - o[1], f))
+
+    def act(o, i, func, scale=1.0, bias=0.0):
+        if bias != 0.0:
+            fn = lambda: sq.activation(ap(o), ap(i), func, bias=bias, scale=scale)
+        else:
+            fn = lambda: sq.activation(ap(o), ap(i), func, scale=scale)
+        return add("scalar", fn, [i], [o], 0.02 + vc(o[2] - o[1], 1.0))
+
+    def ind(win, off):
+        return ap(win).indirect(ap(off))
+
+    def gat(eng, o, win, off):
+        i = len(ops)
+
+        def fn():
+            if ops[i]["eng"] == "scalar":
+                return sq.activation(ap(o), ind(win, off), F.Copy)
+            return vq.tensor_copy(ap(o), ind(win, off))
+        add(eng, fn, [win, off], [o], vc(o[2] - o[1], GA))
+        ops[i]["flex"] = ops[i]["gather"] = True
+
+    def either(eng, o, src, scale=1.0, bias=0.0):
+        i = len(ops)
+
+        def fn():
+            if ops[i]["eng"] == "scalar":
+                if bias == 0.0:
+                    return sq.activation(ap(o), ap(src), F.Copy)
+                return sq.activation(ap(o), ap(src), F.Identity, bias=bias, scale=scale)
+            if bias == 0.0:
+                return vq.tensor_copy(ap(o), ap(src))
+            return vq.tensor_scalar(ap(o), ap(src), scale, bias, A.mult, A.add)
+        add(eng, fn, [src], [o], vc(o[2] - o[1], 1.0))
+        ops[i]["flex"] = True
+
+    def gtt(o, win, off, b, op):
+        add("vector", lambda: vq.tensor_tensor(ap(o), ind(win, off), ap(b), op), [win, off, b], [o], vc(o[2] - o[1], GA))
+        ops[-1]["gather"] = True
+
+    def mset(o, val, step=1):
+        return add("vector", lambda: vq.memset(T[o[0]][:, o[1]:o[2]:step], val), [], [o],
+                   vc((o[2] - o[1]) // step, 0.5 if two(o) else 1.0))
+
+    def mat(kind, name):
+        k = {"F": MF, "B": MB, "H": MH}[kind].index(name)
+        return ("MT" + kind, 128 * k, 128 * k + 128)
+
+    def mm(groups):
+        r, w, cost = [], [], 0.03
+        for o, terms in groups:
+            w.append(o)
+            for l, x, st in terms:
+                r += [l, x]
+                cost += max(64, o[2] - o[1]) * PC * (4 if SCRATCH[x[0]][2] == f32 else 1)
+
+        def fn():
+            last = None
+            for o, terms in groups:
+                for k, (l, x, st) in enumerate(terms):
+                    last = pq.matmul(ap(o), ap(l), T[x[0]][:, x[1]:x[2]:st], k == 0, k == len(terms) - 1)
+            return last
+        return add("tensor", fn, r, w, cost)
+
+    def tolist(o, src, more=()):
+        terms = [(("VI", 128 * i, 128 * i + 128), (src[0], src[1] + i, src[2]), 16) for i in range(16)]
+        return mm([(o, terms + list(more))])
+
+    def dma(q, pairs, r, w, nbytes, accum=False):
+        eng = {"sync": g.sync, "scalar": g.scalar, "g": g}[q]
+
+        def fn(sem):
+            for o, i in pairs():
+                if accum:
+                    eng.dma_start(o, i, accum_op=A.add).then_inc(sem, 16)
+                else:
+                    eng.dma_start(o, i).then_inc(sem, 16)
+        cnt = len(pairs())
+        return add(q, fn, r, w, (1.0 if q == "g" else 0.1) * cnt, 2.0 + nbytes * (2 if accum else 1) / 500e3, "dma", cnt)
+
+    narr = [0]
+
+    def send(items):
+        k = narr[0]
+        narr[0] += 1
+        per = 8 if len(items) <= 2 else 4
+
+        def fn():
+            tr = []
+            for j, (dst, s, l) in enumerate(items):
+                rid, pid, _ = topo.addr(dst)
+                m = 0
+                for e in topo.engines(core, dst)[j * per:(j + 1) * per]:
+                    m |= 1 << e
+                tr.append(RemoteDMATransfer(dst_ids=[DstId(rid=rid, pnc=pid)], dma_engine_mask=m,
+                                            remote_sem=T.sem["arr%d" % k], src=ap(s), dst=ap(l)))
+            g.remote_dma_fused(tr, local_sem=T.sem.sent)
+        i = add("g", fn, [s for _, s, _ in items], [l for _, _, l in items], 1.0, 3.0 if k else 4.5, "net", per * len(items))
+        ops[i]["sem"] = "arr%d" % k
+        return i
+
+    def u(name, a=0, b=K):
+        k = US.index(name) * K
+        return ("U", k + a, k + b)
+
+    def gc(fn, r, w, nel):
+        return add("g", fn, r, w, 0.15 + 2 * nel * CY)
+
+    def turned(o, i, turn, way):
+        if not turn:
+            return [(o[:, :], i)]
+        if way > 0:
+            return [(o[16:128, :], i[0:112, :]), (o[0:16, :], i[112:128, :])]
+        return [(o[0:112, :], i[16:128, :]), (o[112:128, :], i[0:16, :])]
+
+    def rows(t, a, b, c0, c1):
+        return t[a:b, c0:c1]
+
+    def tpairs(ot, oc, it, ic, turn, way):
+        if not turn:
+            return [(rows(ot, 0, 128, *oc), rows(it, 0, 128, *ic))]
+        if way > 0:
+            return [(rows(ot, 16, 128, *oc), rows(it, 0, 112, *ic)), (rows(ot, 0, 16, *oc), rows(it, 112, 128, *ic))]
+        return [(rows(ot, 0, 112, *oc), rows(it, 16, 128, *ic)), (rows(ot, 112, 128, *oc), rows(it, 0, 16, *ic))]
+
+    dma("sync", lambda: tpairs(T.SXB, (0, 256), T.x0, (0, H), turn_l, -1) + tpairs(T.SXB, (256, 512), T.x0, (V - H, V), turn_r, 1),
+        [], [("SXB", 0, 512)], 128 * 1024)
+    dma("scalar", lambda: tpairs(T.SI, (0, 64), T.lf, (K - 64, K), turn_r, 1) + tpairs(T.SI, (64, 128), T.rt, (K - 64, K), turn_r, 1),
+        [], [("SI", 0, 128)], 128 * 512)
+    dma("scalar", lambda: [(T.LI[:, 0:K], T.rt[:, :]), (T.LI[:, K:2 * K], T.lf[:, :])], [], [("LI", 0, 2 * K)], 128 * 1536)
+    dma("sync", lambda: [(T.XB[:, O0:O1], T.x0[:, :])], [], [("XB", O0, O1)], 128 * 6144)
+    send([(left, ("SXB", 0, 256), ("XB", O1, O1 + H)), (right, ("SXB", 256, 512), ("XB", PAD, O0)),
+          (right, ("SI", 0, 128), ("GI", 0, 128))])
+
+    gc(lambda: g.iota(T.KI[:, 0:2], [[0, 2]], 0, 1), [], [("KI", 0, 2)], 2)
+    gc(lambda: g.iota(T.IO[:, :], [[16, CW]], 0, 0, allow_small_or_imprecise_dtypes=True), [], [("IO", 0, CW)], CW)
+    mset(("ONF", 0, K), 1.0)
+    mset(("ONB", 0, K), 1.0)
+    If = mat("F", "I")
+    gc(lambda: g.affine_select(ap(If), T.ONF[:, 0:128], [[-1, 128]], A.is_equal, 0.0, 0, 1), [("ONF", 0, 128)], [If], 128)
+    gc(lambda: g.iota(T.RW[:, :], [[1, O0]], -O0 // 2, 0, allow_small_or_imprecise_dtypes=True), [], [("RW", 0, O0)], O0)
+    ts(("KI", 2, 3), ("KI", 0, 1), 15, None, A.bitwise_and)
+    ts(("KI", 3, 4), ("KI", 0, 1), 4, None, A.arith_shift_right)
+    cp(("KF", 0, 2), ("KI", 2, 4))
+    ts(("KF", 2, 3), ("KF", 0, 1), 0.0, None, A.is_equal)
+    ts(("KF", 3, 4), ("KF", 0, 1), 1.0, float(O0 // 2), A.is_equal, A.mult)
+    ts(("IO", 0, CW), ("IO", 0, CW), T.KF[:, 0:1], None, A.add, extra=[("KF", 0, 1)])
+    for b in ("XB",):
+        mset((b, 0, PAD), FAR)
+        mset((b, WP - PAD, WP), FAR)
+    for o in (0, WP):
+        mset(("XF", o, o + PAD), FAR)
+        mset(("XF", o + WP - PAD, o + WP), FAR)
+
+    def sub(r, a, b):
+        return (r[0], r[1] + a, r[1] + b)
+
+    def scaled(o, c, turn=False, way=0):
+        if not way:
+            act(o, If, F.Copy, scale=c)
+            return
+        a, b = (16, 112) if way > 0 else (112, 16)
+        act(sub(o, a, 128), sub(If, 0, b) if turn else sub(If, a, 128), F.Copy, scale=c)
+        act(sub(o, 0, a), sub(If, b, 128) if turn else sub(If, 0, a), F.Copy, scale=c)
+
+    def strided(o, o0, i0):
+        return add("vector", lambda: vq.tensor_copy(T[o[0]][:, o[1] + o0:o[2]:16], T[If[0]][:, If[1] + i0:If[2]:16]),
+                   [If], [o], vc(8, 1))
+    m = mat("F", "S1p"); cp(sub(m, 1, 128), sub(If, 0, 127)); mset(m, 0.0, 16)
+    m = mat("F", "S2p"); mset(m, 0.0); strided(m, 0, 15)
+    scaled(mat("F", "nI"), -1.0)
+    for nm, c in (("I", 1.0), ("I2", 2.0), ("nI2", -2.0), ("nI", -1.0), ("I3712", float(WP))):
+        scaled(mat("B", nm), c)
+    mset(("VI", 0, 2048), 0.0)
+    for q in range(8):
+        add("vector", lambda q=q: vq.tensor_scalar(T.VI[:, 16 * q:16 * q + 129 * 15 + 1:129], T.ONF[:, 0:16], T.KF[:, 1:2], float(q), A.mult, A.is_equal),
+            [("ONF", 0, 16), ("KF", 1, 2)], [("VI", 0, 2048)], vc(16, 1))
+        ops[-1]["par"] = "vi"
+    m = mat("F", "S1m"); cp(sub(m, 0, 127), sub(If, 1, 128)); mset(sub(m, 15, 128), 0.0, 16)
+    m = mat("F", "S2m"); mset(m, 0.0); strided(m, 15, 0)
+    scaled(mat("F", "I232"), float(CW))
+    scaled(mat("F", "RL"), 1.0, turn_l, -1)
+    scaled(mat("F", "RR"), 1.0, turn_r, 1)
+    scaled(mat("H", "I"), 1.0)
+    scaled(mat("H", "nI3712"), -float(WP))
+    kinds = ["B", "F"] + (["H"] if HALF else [])
+    for kd in kinds:
+        scaled(mat(kd, "P9"), 1.125); scaled(mat(kd, "N1"), -0.125)
+        if kd == "F" and HALF:
+            continue
+        scaled(mat(kd, "P9L"), 1.125, turn_l, -1); scaled(mat(kd, "N1L"), -0.125, turn_l, -1)
+        scaled(mat(kd, "P9R"), 1.125, turn_r, 1); scaled(mat(kd, "N1R"), -0.125, turn_r, 1)
+    for nm, c in (("nI", -1.0), ("I2", 2.0), ("nI2", -2.0)):
+        scaled(mat("H", nm), c)
+    scaled(mat("F", "I2"), 2.0)
+    scaled(mat("F", "nI2"), -2.0)
+    scaled(mat("B", "I7"), 7.0)
+    for b in ("TR", "TL"):
+        gc(lambda b=b: g.iota(T[b][:, :], [[0, WP]], 0, 0, allow_small_or_imprecise_dtypes=True), [], [(b, 0, WP)], WP)
+    for b in ("A2", "A4"):
+        ts((b, 0, O0), ("RW", 0, O0), T.KF[:, 2:3], T.KF[:, 3:4], A.mult, A.add, extra=[("KF", 2, 4)])
+    mset(("HR", 0, 2 * CW), 0.0)
+    mset(("HL", 0, 2 * CW), 0.0)
+    cp(("HA", 0, CW), ("IO", 0, CW))
+    tt(("HA", CW, 2 * CW), ("IO", 0, CW), ("HA", 0, CW), A.subtract)
+    IOo = ("IO", C0, C1)
+
+    def nl(k, t, a, b):
+        return ("N" + k, t * CW + a, t * CW + b)
+
+    for j, k in enumerate("RL"):
+        ts(nl(k, 0, C0, C1), ("LI", j * K, j * K + K), float(PAD), None, A.add)
+        cp(u("e" + k), nl(k, 0, C0, C1))
+    ts(nl("L", 0, C0 - 1, C0), ("GI", 63, 64), float(PAD - V), None, A.add)
+    ts(nl("R", 0, C0 - 1, C0), ("GI", 127, 128), float(PAD - V), None, A.add)
+
+    bank = {"R": "LA", "L": "LB"}
+
+    def cands(t):
+        d = 1 if t % 2 == 0 else -1
+        s1, s2 = (mat("F", "S1p"), mat("F", "S2p")) if d > 0 else (mat("F", "S1m"), mat("F", "S2m"))
+        for k in "RL":
+            sh = [(s1, nl(k, t, C0, C1), 1), (s2, nl(k, t, C0 - d, C1 - d), 1)]
+            mm([((bank[k], 0, K), sh)])
+            if k == "R":
+                ts(u("cR"), (bank[k], 0, K), float(d), float(WP - PAD), A.add, A.min)
+            else:
+                ts(u("cL"), (bank[k], 0, K), float(d), float(PAD - 1), A.add, A.max)
+            mm([((bank[k], K, 2 * K), sh + [(mat("F", "nI"), nl(k, t, C0, C1), 1),
+                                            (mat("F", "I" if d > 0 else "nI"), ("ONF", 0, K), 1)])])
+
+    def table(tab, h):
+        def pairs():
+            out = []
+            for half in range(2):
+                p = 64 * half
+                out.append((T[tab][p:p + 61:20, :], T[h][p:p + 64, 0:CW]))
+                out.append((T[tab][p + 12:p + 49:12, :], T[h][p:p + 64, CW:2 * CW]))
+            return out
+        dma("sync", pairs, [(h, 0, 2 * CW)], [(tab, 0, WP)], 128 * 1000)
+
+    def tabpos(o, src, qm, ps):
+        either("scalar", qm, src, 0.0625, 1024.0 - 0.46875)
+        mm([(ps, [(mat("F", "I232"), src, 1), (mat("H", "nI3712"), qm, 1), (mat("H", "I"), qm, 1)])])
+        ts(o, ps, float((WP - 1) * 1024), None, A.add)
+
+    def hilo(h, src, a, b, e, ps=None):
+        either(ENG[e], (h, a, b), src)
+        if ps:
+            mm([((ps, 0, b - a), [(mat("F", "I"), src, 1), (mat("B", "nI"), (h, a, b), 1)])])
+            either(ENG[e], (h, CW + a, CW + b), (ps, 0, b - a))
+        else:
+            tt((h, CW + a, CW + b), src, (h, a, b), A.subtract)
+
+    nse = [0]
+
+    def edges(t, what, bk):
+        gr, items = [], []
+        for m, (k, way) in enumerate(what):
+            ps, se = (bk, 384 + 16 * m, 400 + 16 * m), ("SE", nse[0], nse[0] + 16)
+            nse[0] += 16
+            if way < 0:
+                gr.append((ps, [(mat("F", "RL"), nl(k, t + 1, C0, C0 + 16), 1)]))
+                items.append((left, se, nl(k, t + 1, C1, C1 + 16)))
+            else:
+                gr.append((ps, [(mat("F", "RR"), nl(k, t + 1, C1 - 16, C1), 1)]))
+                items.append((right, se, nl(k, t + 1, C0 - 16, C0)))
+        mm(gr)
+        for (ps, _), (k, way), it in zip(gr, what, items):
+            either("scalar", it[1], ps, 1.0, -float(way * V))
+        send(items)
+
+    qn = [0]
+
+    def qslot():
+        qn[0] += 1
+        return "QA" if qn[0] % 2 else "QB"
+    en = [0]
+
+    def eslot():
+        en[0] += 1
+        return "E0" if en[0] % 2 else "E1"
+
+    XS = [("XB", 0), ("XF", WP), ("XF", 0)]
+    cands(0)
+    for t in range(RO):
+        xb, xo = XS[t]
+        kd = KD[t]
+        win = (xb, xo, xo + WP)
+
+        def xown(a, b):
+            return (xb, xo + O0 + a, xo + O0 + b)
+
+        def xpe(a, b):
+            return ("XH", a, b) if kd == "H" else xown(a, b)
+
+        def xc(a, b):
+            return ("XH", a, b) if kd == "H" else (xb, xo + WP + O0 + a, xo + WP + O0 + b)
+        gen, ppn, wb = {"B": ("GE", "PP", "GE"), "H": ("GH", "PH", "GH"), "F": ("FA", "FB", "DW")}[kd]
+
+        def ring(nm, a, b):
+            return (nm, a % 2048, a % 2048 + b - a) if nm in ("FA", "FB") else (nm, a, b)
+
+        def ge(a, b):
+            return ring(gen, a, b)
+
+        def pp(a, b):
+            return ring(ppn, a, b)
+        last = t == RO - 1
+        for c in range(3):
+            a, b = 1024 * c, 1024 * c + 1024
+            if kd == "H":
+                either("scalar", xc(a, b), xown(a, b))
+            elif t:
+                dma("sync", lambda o=xc(a, b), i=xown(a, b): [(ap(o), ap(i))], [xown(a, b)], [xc(a, b)], 512 * 1024)
+        if t == 0:
+            dma("sync", lambda o=xc(0, V): [(ap(o), T.x0[:, :])], [], [xc(0, V)], 128 * 6144)
+        dma("g" if xb == "XB" else "sync",
+            lambda xb=xb, xo=xo: [(T.MA[:, 0:O0], T[xb][:, xo:xo + O0]), (T.MB[:, 0:O0], T[xb][:, xo:xo + O0])],
+            [(xb, xo, xo + O0)], [("MA", 0, O0), ("MB", 0, O0)], 128 * 2560)
+        dma("sync", lambda xb=xb, xo=xo: [(T[xb][:, xo + WP:xo + WP + O0], T[xb][:, xo:xo + O0])],
+            [(xb, xo, xo + O0)], [(xb, xo + WP, xo + WP + O0)], 128 * 1280)
+        for j, k in enumerate("RL"):
+            bk = bank[k]
+            for nc, c in enumerate((2, 0, 1) if k == "R" else (0, 1, 2)):
+                a, b = 1024 * c, 1024 * c + 1024
+                ue, uc = u("e" + k, 64 * c, 64 * c + 64), u("c" + k, 64 * c, 64 * c + 64)
+                q = qslot()
+                form = OPT["form"][t][3 * j + c]
+                r0 = 1024 * (3 * j + nc) if kd == "F" else a
+                g1, p1 = ge(r0, r0 + 1024), pp(r0, r0 + 1024)
+                more = []
+                if form == "a":
+                    gtt(g1, win, uc, xc(a, b), A.subtract)
+                    gtt(p1, win, ue, xc(a, b), A.subtract)
+                    act((q, 0, 1024), g1, F.Abs)
+                    act(p1, p1, F.Abs)
+                    tt(("NE", a, b), (q, 0, 1024), p1, A.is_lt)
+                elif form == "c":
+                    gat("scalar", g1, win, uc)
+                    gtt(p1, win, ue, xc(a, b), A.subtract)
+                    mm([((q, s, s + 512), [(mat(kd, "I"), sub(g1, s, s + 512), 1), (mat(kd, "nI"), xpe(a + s, a + s + 512), 1)]) for s in (0, 512)])
+                    act((q, 0, 1024), (q, 0, 1024), F.Abs)
+                    act(p1, p1, F.Abs)
+                    tt(("NE", a, b), (q, 0, 1024), p1, A.is_lt)
+                else:
+                    gat("scalar", g1, win, ue)
+                    gtt(p1, win, uc, g1, A.subtract)
+                    mm([((q, s, s + 512), [(mat(kd, "I2"), sub(g1, s, s + 512), 1), (mat(kd, "nI2"), xpe(a + s, a + s + 512), 1),
+                                           (mat(kd, "I"), sub(p1, s, s + 512), 1)]) for s in (0, 512)])
+                    tt(("NE", a, b), (q, 0, 1024), p1, A.mult)
+                    if form == "v":
+                        ts(("NE", a, b), ("NE", a, b), 0.0, None, A.is_lt)
+                    else:
+                        act(("NE", a, b), ("NE", a, b), F.Sign, scale=-1.0, bias=-2.0 ** -26)
+                        more = [(mat("B", "I7"), ("ONB", 0, 64), 1)]
+                tolist((bk, 64 * c, 64 * c + 64), ("NE", a, b), more)
+                if (k, c) not in GROUPS:
+                    continue
+                ca, cb = GROUPS[k, c]
+                tv = ("TT", j * K + ca, j * K + cb)
+                new = nl(k, t + 1, C0 + ca, C0 + cb)
+                ts(tv, (bk, ca, cb), 8.5, None, A.is_ge)
+                tt((bk, K + ca, K + cb), (bk, K + ca, K + cb), tv, A.mult)
+                tt(new, (bk, K + ca, K + cb), nl(k, t, C0 + ca, C0 + cb), A.add)
+                if k == "R" and cb == K:
+                    edges(t, [("R", 1)], bk)
+                tabpos(u("t" + k, ca, cb), new, ("QM", j * K + ca, j * K + cb), (bk, ca, cb))
+                if k == "R" or not last:
+                    cp(u("e" + k, ca, cb), new)
+            if k == "L":
+                edges(t, [("L", -1)] + ([] if last else [("L", 1)] if t % 2 else [("R", -1)]), bk)
+            a, b = (C0 - 16, C1) if k == "R" else (C0, C1 + 16)
+            hilo("H" + k, nl(k, t + 1, a, b), a, b, OPT["hi"][t][j], bk if LOPE[j] else None)
+            table("T" + k, "H" + k)
+        for c in range(3):
+            a, b = 1024 * c, 1024 * c + 1024
+            ue = u("eR", 64 * c, 64 * c + 64)
+            if OPT["w"][t][c] == "s":
+                gat("scalar", (wb, a, b), win, ue)
+                for s in (a, a + 512):
+                    e = eslot()
+                    mm([((e, 0, 512), [(mat(kd, "I"), (wb, s, s + 512), 1), (mat(kd, "nI"), xpe(s, s + 512), 1)])])
+                    act(("DW", s, s + 512), (e, 0, 512), F.Abs)
+            else:
+                gtt(("DW", a, b), win, ue, xc(a, b), A.subtract)
+                act(("DW", a, b), ("DW", a, b), F.Abs)
+        hv = [(s, s + V // PARTS[t]) for s in range(0, V, V // PARTS[t])]
+        pw = K // PARTS[t]
+
+        def eng(nm, h):
+            return ENG[OPT[nm][t][h]]
+
+        def mstep(src, lst, first, nxt):
+            for a, b in hv:
+                gtt(("MP", a, b), (src[0], src[1], src[1] + O0 + b), u(lst, a // 16, b // 16), xc(a, b) if first else ("MP", a, b), A.max)
+            if nxt:
+                for a, b in hv:
+                    dma("sync", lambda a=a, b=b: [(T[nxt][:, O0 + a:O0 + b], T.MP[:, a:b])], [("MP", a, b)], [(nxt, O0 + a, O0 + b)], 512 * (b - a))
+        for h, (a, b) in enumerate(hv):
+            gat(eng("rl", h), ("A4", O0 + a, O0 + b), ("TR", 0, WP), u("tL", a // 16, b // 16))
+            tolist(("LA", a // 16, b // 16), ("A4", O0 + a, O0 + b))
+        tt(("LA", 0, K), ("LA", 0, K), IOo, A.not_equal)
+        tt(("LA", 0, K), ("LA", 0, K), IOo, A.mult)
+        tt(("NA", 0, K), ("LA", 0, K), nl("L", t + 1, C0, C1), A.max)
+        hilo("HA", ("NA", 0, K), C0, C1, OPT["hi"][t][2], "LA" if LOPE[2] else None)
+        table("TR", "HA")
+        tabpos(u("ta"), ("NA", 0, K), ("QM", 2 * K, 3 * K), ("LA", 0, K))
+        cp(u("a1"), ("NA", 0, K))
+        for h, (a, b) in enumerate(hv):
+            gat(eng("lr", h), ("NE", a, b), ("TL", 0, WP), u("tR", a // 16, b // 16))
+        tolist(("LB", 0, K), ("NE", 0, V))
+        tt(("EN", 0, K), ("LB", 0, K), IOo, A.not_equal)
+        mstep((xb, xo), "a1", True, "MA")
+        for h, (a, b) in enumerate(hv):
+            ca, cb = a // 16, b // 16
+            ps = ("LB" if h % 2 else "LA", 0, pw)
+            gat(eng("a2", h), ("A2", O0 + a, O0 + b), ("TR", 0, WP), u("ta", ca, cb))
+            tolist(ps, ("A2", O0 + a, O0 + b))
+            cp(u("a2", ca, cb), ps)
+            tt(("HH", ca, cb), ps, ("EN", ca, cb), A.mult)
+        mstep(("MA", 0), "a2", False, "MB")
+        for h, (a, b) in enumerate(hv):
+            ca, cb = a // 16, b // 16
+            ps = ("LB" if (h + PARTS[t]) % 2 else "LA", 0, pw)
+            gat(eng("a4", h), ("A4", O0 + a, O0 + b), ("A2", 0, O0 + b), u("a2", ca, cb))
+            tolist(ps, ("A4", O0 + a, O0 + b))
+            cp(u("a4", ca, cb), ps)
+            tt(("GO", ca, cb), ps, ("HH", ca, cb), A.is_lt)
+        mstep(("MB", 0), "a4", False, "MA")
+        for h, (a, b) in enumerate(hv):
+            ca, cb = a // 16, b // 16
+            ps = ("LB" if h % 2 else "LA", 0, pw)
+            gat(eng("a8", h), ("A2", O0 + a, O0 + b), ("A4", 0, O0 + b), u("a4", ca, cb))
+            tolist(ps, ("A2", O0 + a, O0 + b), [(mat("B", "I3712"), ("ONB", 0, pw), 1)])
+            ts(u("a8", ca, cb), ps, -float(WP), None, A.add)
+            tt(ps, ps, ("GO", ca, cb), A.mult)
+            tt(ps, ps, ("IO", C0 + ca, C0 + cb), A.max)
+            cp(u("s", ca, cb), ps)
+        if not last:
+            cands(t + 1)
+        for h, (a, b) in enumerate(hv):
+            gat(eng("x8", h), (xb, xo + WP + O0 + a, xo + WP + O0 + b), (xb, xo, xo + O0 + b), u("a8", a // 16, b // 16))
+        nxs = [0]
+
+        def xs(a, b):
+            gat(eng("xs", nxs[0]), ge(a, b), (xb, xo, xo + WP + O0 + b), u("s", a // 16, b // 16))
+            nxs[0] += 1
+
+        def zz(o, a, b, sfx):
+            return (o, [(mat(kd, "P9" + sfx), xpe(a, b), 1), (mat(kd, "N1" + sfx), ge(a, b), 1)])
+        if not last:
+            nb, no = XS[t + 1]
+            xs(0, H)
+            xs(V - H, V)
+            q = qslot()
+            mm([zz((q, 0, H), 0, H, "L"), zz((q, H, 2 * H), V - H, V, "R")])
+            sx = 512 * t
+            ts(("SXF", sx, sx + 512), (q, 0, 512), 0.0, 4.0, A.max, A.min)
+            send([(left, ("SXF", sx, sx + H), (nb, no + O1, no + O1 + H)), (right, ("SXF", sx + H, sx + 512), (nb, no + PAD, no + O0))])
+            for a, b in ((H, 1024), (1024, 2048), (2048, V - H)):
+                xs(a, b)
+            mv = [(0, 1024), (1024, 2048), (2048, V)]
+        else:
+            mv = [(0, 1024), (1024, 2048), (2048, 2560), (2560, V)]
+        for a, b in mv:
+            if last:
+                xs(a, b)
+            q = qslot()
+            mm([zz((q, s - a, s - a + 512), s, s + 512, "") for s in range(a, b, 512)])
+            if last:
+                ts(pp(a, b), (q, 0, b - a), 0.0, 4.0, A.max, A.min)
+                dma("sync", lambda a=a, b=b, i=pp(a, b): [(T.xe[:, a:b], ap(i))], [pp(a, b)], [], 512 * (b - a))
+            else:
+                ts((nb, no + O0 + a, no + O0 + b), (q, 0, b - a), 0.0, 4.0, A.max, A.min)
+        mstep(("MA", 0), "a8", False, None)
+        ends = [1536, V] if not last else [1024, 2048, 2560, V]
+        s0 = 0
+        for s in range(0, V, 512):
+            e = eslot()
+            act((e, 0, 512), ("DW", s, s + 512), F.Exp, scale=-1.0)
+            tt(("MP", s, s + 512), (e, 0, 512), ("MP", s, s + 512), A.mult)
+            if s + 512 in ends:
+                dma("g" if t else "sync", lambda a=s0, b=s + 512: [(T.ye[:, a:b], T.MP[:, a:b])], [("MP", s0, s + 512)],
+                    [("ye", s0, s + 512)], 512 * (s + 512 - s0), accum=t > 0)
+                s0 = s + 512
+    return ops
+
+
+def depends(ops):
+    seen = {}
+    deps = []
+    for i, o in enumerate(ops):
+        d = set()
+        acc = [(r, False) for r in o["r"]] + [(w, True) for w in o["w"]]
+        for (nm, a, b), wr in acc:
+            for j, a2, b2, wr2 in seen.get(nm, ()):
+                if nm in PSUM and (ops[j]["eng"] != o["eng"] or o.get("flex") or ops[j].get("flex")):
+                    d.add(j)
+                elif (wr or wr2) and a < b2 and a2 < b:
+                    if not (o.get("par") and o.get("par") == ops[j].get("par")):
+                        d.add(j)
+        for (nm, a, b), wr in acc:
+            seen.setdefault(nm, []).append((i, a, b, wr))
+        d.discard(i)
+        deps.append(d)
+    return deps
+
+
+def schedule(ops, deps):
+    n = len(ops)
+    kids = [[] for _ in range(n)]
+    for i in range(n):
+        for j in deps[i]:
+            kids[j].append(i)
+    cost = [o["cost"] for o in ops]
+    lat = [o["lat"] for o in ops]
+    engs = [o["eng"] for o in ops]
+
+    def one(pre, post, pr, back, slack):
+        left = [len(d) for d in pre]
+        ready = [lat[i] if back else 0.0 for i in range(n)]
+        pool = {}
+        for i in range(n):
+            if not left[i]:
+                pool.setdefault(engs[i], []).append(i)
+        free, order, start, fin = {}, {}, [0.0] * n, [0.0] * n
+        for _ in range(n):
+            best = None
+            for e, lst in pool.items():
+                if not lst:
+                    continue
+                t0 = max(free.get(e, 0.0), min(ready[i] for i in lst))
+                if best is None or t0 < best[0]:
+                    best = (t0, e)
+            t0, e = best
+            i = max((i for i in pool[e] if ready[i] <= t0 + slack), key=lambda i: pr[i])
+            pool[e].remove(i)
+            start[i] = max(free.get(e, 0.0), ready[i])
+            free[e] = fin[i] = start[i] + cost[i]
+            order.setdefault(e, []).append(i)
+            for k in post[i]:
+                ready[k] = max(ready[k], fin[i] + HOP + (lat[k] if back else lat[i]))
+                left[k] -= 1
+                if not left[k]:
+                    pool.setdefault(engs[k], []).append(k)
+        return order, start, fin
+    pr0 = [0.0] * n
+    for i in range(n - 1, -1, -1):
+        pr0[i] = cost[i] + lat[i] + max([pr0[k] + HOP for k in kids[i]] + [0.0])
+    best = None
+    for slack in SLACK:
+        pr = pr0
+        for _ in range(PASSES):
+            order, start, fin = one(deps, kids, pr, False, slack)
+            end = [fin[i] + lat[i] for i in range(n)]
+            if best is None or max(end) < max(best[2]):
+                best = (order, start, end, kids)
+            pr = one(kids, deps, fin, True, slack)[2]
+    seq = sorted(range(n), key=lambda i: (best[1][i], i))
+    anc = [0] * n
+    red = []
+    for i in range(n):
+        far = 0
+        for j in deps[i]:
+            far |= anc[j]
+        red.append([j for j in deps[i] if not far >> j & 1])
+        anc[i] = far
+        for j in deps[i]:
+            anc[i] |= 1 << j
+    des = [0] * n
+    for i in range(n - 1, -1, -1):
+        for k in kids[i]:
+            des[i] |= des[k] | 1 << k
+    names = ["vector", "scalar", "tensor", "sync", "g"]
+    en = [names.index(e) for e in engs]
+    flex = [i for i in range(n) if ops[i].get("flex")]
+    after = [lat[i] + HOP for i in range(n)]
+    costs = [cost] + [[o["cost"] * (f if o.get("gather") else 1.0) * (h if o["eng"] == "tensor" else 1.0) for o in ops] for f, h in ALT]
+
+    def run(seq, en, cost, why=None):
+        free = [0.0] * 5
+        who = [-1] * 5
+        fin = [0.0] * n
+        top = 0.0
+        for i in seq:
+            e = en[i]
+            s = free[e]
+            w = who[e]
+            for j in red[i]:
+                r = fin[j] + after[j]
+                if r > s:
+                    s = r
+                    w = j
+            s += cost[i]
+            free[e] = fin[i] = s
+            who[e] = i
+            if why is not None:
+                why[i] = w
+            if s + lat[i] > top:
+                top = s + lat[i]
+        return top, fin
+
+    def score(seq, en):
+        return sum(run(seq, en, c)[0] for c in costs) / len(costs)
+    x = [SEED]
+
+    def rnd(m):
+        x[0] = (x[0] * 6364136223846793005 + 1442695040888963407) % 18446744073709551616
+        return (x[0] >> 33) % m
+    cur = score(seq, en)
+    top = (cur, list(seq), list(en))
+    path = []
+    for it in range(TRIES):
+        if it % 20 == 0:
+            why = [-1] * n
+            fin = run(seq, en, costs[rnd(len(costs))], why)[1]
+            i = max(range(n), key=lambda i: fin[i] + lat[i])
+            path = []
+            while i >= 0:
+                path.append(i)
+                i = why[i]
+        kind = rnd(10)
+        en2, seq2 = en, seq
+        if kind == 0:
+            i = flex[rnd(len(flex))]
+            en2 = list(en)
+            en2[i] = 1 - en2[i]
+        else:
+            i = path[rnd(len(path))] if kind < 7 else rnd(n)
+            if kind % 2 == 0 and why[i] >= 0 and en[why[i]] == en[i]:
+                i = why[i]
+            p = seq.index(i)
+            far = 1 + rnd(4) * rnd(12) + rnd(4)
+            if kind % 2:
+                q = max(0, p - far)
+                m = anc[i]
+                seq2 = seq[:q] + [j for j in seq[q:p] if m >> j & 1] + [i] + [j for j in seq[q:p] if not m >> j & 1] + seq[p + 1:]
+            else:
+                q = p + 1 + far
+                m = des[i]
+                seq2 = seq[:p] + [j for j in seq[p + 1:q] if not m >> j & 1] + [i] + [j for j in seq[p + 1:q] if m >> j & 1] + seq[q:]
+            if kind == 5 and ops[i].get("flex"):
+                en2 = list(en)
+                en2[i] = 1 - en2[i]
+        v = score(seq2, en2)
+        if v <= cur + TEMP * (1.0 - it / TRIES) * rnd(1000) / 1000.0:
+            cur, seq, en = v, seq2, en2
+            if v < top[0]:
+                top = (v, list(seq), list(en))
+    _, seq, en = top
+    fin = run(seq, en, cost)[1]
+    order = {}
+    for i in seq:
+        order.setdefault(names[en[i]], []).append(i)
+    return order, [fin[i] - cost[i] for i in range(n)], [fin[i] + lat[i] for i in range(n)], kids
+
+
+PLAN = []
+
+
+def rank_program(g, core, T, topo):
+    rank = T.rank_of(core)
+    if rank is None:
+        return
+    ops = build(g, core, T, topo)
+    deps = depends(ops)
+    if not PLAN:
+        PLAN.append(schedule(ops, deps))
+    order, start, end, kids = PLAN[0]
+    for e, lst in order.items():
+        for i in lst:
+            ops[i]["eng"] = e
+    queue = {"vector": g.vector, "scalar": g.scalar, "tensor": g.tensor, "sync": g.sync, "g": g}
+    mark, total, nd, sent = {}, {}, 0, 0
+    for e, lst in order.items():
+        for i in lst:
+            o = ops[i]
+            if o["kind"] == "dma":
+                mark[i] = ("d%d" % nd, 16 * o["cnt"])
+                nd += 1
+            elif o["kind"] == "net":
+                mark[i] = (o["sem"], o["cnt"])
+                sent += o["cnt"]
+            elif kids[i]:
+                s = "gcomp" if e == "g" else e
+                mark[i] = (s, total.get(s, 0) + 1)
+            if i in mark:
+                total[mark[i][0]] = mark[i][1]
+    for e, lst in order.items():
+        q, seen = queue[e], {}
+        for i in lst:
+            o = ops[i]
+            need = {}
+            for j in deps[i]:
+                if e == "tensor" and ops[j]["eng"] == "tensor":
+                    continue
+                s, c = mark[j]
+                if c > seen.get(s, 0) and c > need.get(s, 0):
+                    need[s] = c
+            for s, c in need.items():
+                q.wait_ge(T.sem[s], c)
+                seen[s] = c
+            if o["kind"] == "dma":
+                o["fn"](T.sem[mark[i][0]])
+            elif o["kind"] == "net":
+                o["fn"]()
+            else:
+                ins = o["fn"]()
+                if i in mark:
+                    ins.then_inc(T.sem[mark[i][0]], 1)
+    for s, c in total.items():
+        g.wait_ge(T.sem[s], c)
+    g.wait_ge(T.sem.sent, sent)

@@ -10,65 +10,68 @@ O1 = O0 + V
 WP = O1 + H + PAD
 C0, C1, CW = O0 // 16, O1 // 16, WP // 16
 K = V // 16
+TW = K + 16
+TN = 16 * TW
 FAR = 16.0
+QO = 1280.0
+QC, LC = 118.0, 8.0
+UQ, UL, ZS = 2.0 ** -21, 2.0 ** -20, 4096.0
+TOP = 3700.0
+HI, LO = slice(0, 127, 18), slice(15, 114, 14)
 
 KD = "BHF"
 OPT = {
-    "form": ["ssssss", "ssssss", "acacac"],
-    "w": ["svs", "svs", "svs"],
-    "rl": ["svs", "svs", "svs"], "lr": ["sss", "sss", "sss"],
-    "a2": ["sss", "sss", "sss"], "a4": ["sss", "sss", "sss"], "a8": ["sss", "sss", "sss"],
-    "x8": ["sss", "sss", "sss"], "xs": ["sssss", "sssss", "sssss"],
-    "hi": ["sss", "sss", "sss"],
+    "order": ["R2 L0 R0 R1 L1 L2"] * 3,
+    "form": ["pppppp", "pppppp", "aacaac"],
+    "w": ["sss", "sss", "sss"],
+    "mparts": [3, 3, 3],
+    "rl": ["svs", "sss", "sss"], "a1ends": [[V]] * 3,
+    "a2": ["ss"] * 3, "a4": ["ss"] * 3, "a8": ["ss"] * 3, "x8": ["ss"] * 3, "xs": ["sssss"] * 3,
+    "lope": (1, 0), "slots": ["QA", "QB", "QE"],
+    "groups": [{("R", 2): (128, 192), ("R", 1): (0, 128), ("L", 0): (0, 64), ("L", 2): (64, 192)}] * 3,
 }
-PARTS = [2, 2, 2]
-LOPE = (1, 1, 0)
-GROUPS = {("R", 2): (128, 192), ("R", 1): (0, 128), ("L", 1): (0, 128), ("L", 2): (128, 192)}
-SLACK, PASSES, TRIES, TEMP, SEED, ALT = (0.8,), 3, 70000, 0.6, 1, [(0.85, 1.7)]
+SLACK, PASSES, TRIES, TEMP, SEED, LOAD, FAROFF = 0.3, 1, 120000, 0.0015, 1, 0.4, 8
+SPEEDS = [(1.05, 1.15, 0.00046, 0.15, 2.0, 3.0, 1.0), (1.0, 1.56, 0.00044, 0.12, 2.2, 3.5, 1.0),
+          (1.4, 1.15, 0.00062, 0.2, 2.5, 4.0, 1.2), (1.4, 1.95, 0.0006, 0.15, 2.2, 3.5, 1.0)]
+CY = 0.00083
 
 f32, b16, f16, i32, u16 = "float32", "bfloat16", "float16", "int32", "uint16"
 US = ["eR", "eL", "cR", "cL", "tR", "tL", "a1", "ta", "a2", "a4", "a8", "s"]
-MF = ["I", "nI", "S1p", "S2p", "S1m", "S2m", "I232", "RL", "RR", "P9", "N1", "I2", "nI2"]
-MB = ["I", "nI", "I2", "nI2", "P9", "N1", "P9L", "N1L", "P9R", "N1R", "I3712", "I7"]
-MH = ["I", "nI3712", "nI", "I2", "nI2", "P9", "N1", "P9L", "N1L", "P9R", "N1R"]
-HALF = True
-ENG = {"s": "scalar", "v": "vector"}
+MF = ["I", "nI", "Ih", "S1p", "S2p", "S1m", "S2m", "D1p", "D1m", "ITW", "RL", "RR", "P9", "N1"]
+MB = ["I", "nI", "P9", "P9L", "P9R"]
+MH = ["I", "nI", "Ih", "nTN", "n16", "P9", "N1", "P9L", "N1L", "P9R", "N1R"]
 
 SCRATCH = {
     "XB": ("sbuf", [128, WP + O1], b16),
     "XF": ("sbuf", [128, 2 * WP + O1], f32),
+    "XP": ("sbuf", [128, TN], f32), "XH": ("sbuf", [128, V], f16),
     "MA": ("sbuf", [128, O1], f32), "MB": ("sbuf", [128, O1], f32),
-    "TR": ("sbuf", [128, WP], b16), "TL": ("sbuf", [128, WP], b16),
+    "TR": ("sbuf", [128, TN], b16),
     "A2": ("sbuf", [128, O1], b16), "A4": ("sbuf", [128, O1], b16),
-    "FA": ("sbuf", [128, 2048], f32), "FB": ("sbuf", [128, 2048], f32),
+    "FA": ("sbuf", [128, V], f32), "FB": ("sbuf", [128, V], f32),
     "DW": ("sbuf", [128, V], f32), "MP": ("sbuf", [128, V], f32),
-    "GE": ("sbuf", [128, V], b16), "PP": ("sbuf", [128, V], b16),
-    "NE": ("sbuf", [128, V], b16),
-    "VI": ("sbuf", [128, 2048], b16),
+    "GH": ("sbuf", [128, V], f16), "PH": ("sbuf", [128, V], f16),
+    "NE": ("sbuf", [128, 4096], b16),
+    "VI": ("sbuf", [128, 144], b16), "VP": ("sbuf", [128, 144], f32), "PR": ("sbuf", [128, 136], b16),
+    "PV": ("sbuf", [128, 2 * K], b16), "FL": ("sbuf", [128, 2 * K], b16),
     "U": ("sbuf", [128, K * len(US)], u16),
     "NR": ("sbuf", [128, 4 * CW], f32), "NL": ("sbuf", [128, 4 * CW], f32),
-    "HR": ("sbuf", [128, 2 * CW], b16), "HL": ("sbuf", [128, 2 * CW], b16), "HA": ("sbuf", [128, 2 * CW], b16),
-    "NA": ("sbuf", [128, K], f32), "TT": ("sbuf", [128, 2 * K], f32), "QM": ("sbuf", [128, 3 * K], f16),
+    "HR": ("sbuf", [128, 2 * TW], b16), "HA": ("sbuf", [128, 2 * TW], b16), "HL": ("sbuf", [128, 2 * TW], f32),
+    "NA": ("sbuf", [128, K], f32), "TT": ("sbuf", [128, 2 * K], f32), "QM": ("sbuf", [128, 3 * TW], f16),
     "EN": ("sbuf", [128, K], f32), "HH": ("sbuf", [128, K], f32), "GO": ("sbuf", [128, K], f32),
-    "IO": ("sbuf", [128, CW], f32), "ONF": ("sbuf", [128, K], f32), "ONB": ("sbuf", [128, K], b16),
+    "IO": ("sbuf", [128, CW], f32), "ONF": ("sbuf", [128, 128], f32), "CB": ("sbuf", [128, 4 * K], b16),
     "LI": ("sbuf", [128, 2 * K], i32), "SI": ("sbuf", [128, 128], i32), "GI": ("sbuf", [128, 128], i32),
-    "SXB": ("sbuf", [128, 512], b16), "SXF": ("sbuf", [128, 1024], f32), "SE": ("sbuf", [128, 6 * 32], f32),
+    "SXB": ("sbuf", [128, 512], b16), "SXF": ("sbuf", [128, 1024], f32), "SE": ("sbuf", [128, 8 * 16], f32),
     "MTF": ("sbuf", [128, 128 * len(MF)], f32), "MTB": ("sbuf", [128, 128 * len(MB)], b16),
-    "MTH": ("sbuf", [128, 128 * (len(MH) if HALF else 2)], f16),
-    "KI": ("sbuf", [128, 8], i32), "KF": ("sbuf", [128, 8], f32), "RW": ("sbuf", [128, O0], f32),
+    "MTH": ("sbuf", [128, 128 * len(MH)], f16),
+    "KI": ("sbuf", [128, 8], i32), "KF": ("sbuf", [128, 16], f32), "RW": ("sbuf", [128, O0], f32),
     "QA": ("psum", [128, 1024], f32), "QB": ("psum", [128, 1024], f32),
-    "E0": ("psum", [128, 512], f32), "E1": ("psum", [128, 512], f32),
+    "QE": ("psum", [128, 1024], f32),
     "LA": ("psum", [128, 512], f32), "LB": ("psum", [128, 512], f32),
 }
-if HALF:
-    SCRATCH["GH"] = ("sbuf", [128, V], f16)
-    SCRATCH["PH"] = ("sbuf", [128, V], f16)
-    SCRATCH["XH"] = ("sbuf", [128, V], f16)
-PSUM = ("QA", "QB", "E0", "E1", "LA", "LB")
+PSUM = ("QA", "QB", "QE", "LA", "LB")
 NDMA = 100
-SEMAPHORES = ["vector", "scalar", "tensor", "gcomp", "sent"] + ["arr%d" % k for k in range(12)] + ["d%d" % k for k in range(NDMA)]
-
-CY, GA, PC, HOP = 0.00083 * 1.25, 1.56, 0.00042 * 1.25, 0.1
+SEMAPHORES = ["vector", "scalar", "tensor", "gcomp", "sent"] + ["arr%d" % k for k in range(14)] + ["d%d" % k for k in range(NDMA)]
 
 
 def build(g, core, T, topo):
@@ -79,112 +82,131 @@ def build(g, core, T, topo):
     ops = []
     vq, sq, pq = g.vector, g.scalar, g.tensor
 
-    def ap(r):
-        return T[r[0]][:, r[1]:r[2]]
+    def ap(r, step=1):
+        return T[r[0]][:, r[1]:r[2]:step] if step > 1 else T[r[0]][:, r[1]:r[2]]
 
-    def add(eng, fn, r, w, cost, lat=0.0, kind="c", cnt=1):
-        ops.append(dict(eng=eng, fn=fn, r=list(r), w=list(w), cost=cost, lat=lat, kind=kind, cnt=cnt))
-        return len(ops) - 1
+    def sub(r, a, b):
+        return (r[0], r[1] + a, r[1] + b)
 
-    def two(r):
-        return SCRATCH[r[0]][2] in (b16, f16, u16)
+    def add(alts, r, w, kind="c", cnt=1, nbytes=0):
+        i = len(ops)
+        o = dict(eng=list(alts)[0], alts=alts, r=list(r), w=list(w), kind=kind, cnt=cnt, nbytes=nbytes)
+        o["fn"] = lambda *a: alts[o["eng"]][0](*a)
+        ops.append(o)
+        return i
 
-    def vc(nel, f):
-        return 0.06 + max(64, nel * f) * CY
+    def two(*rs):
+        return all(SCRATCH[r[0]][2] in (b16, f16, u16) for r in rs)
+
+    def onv(fn, nel, f=1.0, kind="c"):
+        return (fn, 0.06, max(64, nel * f), kind)
+
+    def ons(fn, nel, kind="c"):
+        return (fn, 0.08, max(64, nel), kind)
+
+    def ong(fn, nel):
+        return (fn, 0.17, 2 * nel, "c")
 
     def ts(o, i, s1, s2, o0, o1=None, extra=()):
-        f = 0.5 if two(o) and two(i) else 1.0
         if o1 is None:
             fn = lambda: vq.tensor_scalar(ap(o), ap(i), s1, None, o0)
         else:
             fn = lambda: vq.tensor_scalar(ap(o), ap(i), s1, s2, o0, o1)
-        return add("vector", fn, [i] + list(extra), [o], vc(o[2] - o[1], f))
+        return add({"vector": onv(fn, o[2] - o[1], 0.5 if two(o, i) else 1.0)}, [i] + list(extra), [o])
 
     def cp(o, i):
-        f = 0.5 if two(o) and two(i) else 1.0
-        return add("vector", lambda: vq.tensor_copy(ap(o), ap(i)), [i], [o], vc(o[2] - o[1], f))
+        return add({"vector": onv(lambda: vq.tensor_copy(ap(o), ap(i)), o[2] - o[1], 0.5 if two(o, i) else 1.0)}, [i], [o])
 
     def tt(o, a, b, op):
         f = 1.0 if a[0] in PSUM or b[0] in PSUM else 2.0
-        return add("vector", lambda: vq.tensor_tensor(ap(o), ap(a), ap(b), op), [a, b], [o], vc(o[2] - o[1], f))
+        return add({"vector": onv(lambda: vq.tensor_tensor(ap(o), ap(a), ap(b), op), o[2] - o[1], f)}, [a, b], [o])
 
-    def act(o, i, func, scale=1.0, bias=0.0):
-        if bias != 0.0:
-            fn = lambda: sq.activation(ap(o), ap(i), func, bias=bias, scale=scale)
-        else:
-            fn = lambda: sq.activation(ap(o), ap(i), func, scale=scale)
-        return add("scalar", fn, [i], [o], 0.02 + vc(o[2] - o[1], 1.0))
+    def act(o, i, func, scale=1.0):
+        return add({"scalar": ons(lambda: sq.activation(ap(o), ap(i), func, scale=scale), o[2] - o[1])}, [i], [o])
 
     def ind(win, off):
         return ap(win).indirect(ap(off))
 
-    def gat(eng, o, win, off):
-        i = len(ops)
-
-        def fn():
-            if ops[i]["eng"] == "scalar":
-                return sq.activation(ap(o), ind(win, off), F.Copy)
-            return vq.tensor_copy(ap(o), ind(win, off))
-        add(eng, fn, [win, off], [o], vc(o[2] - o[1], GA))
-        ops[i]["flex"] = ops[i]["gather"] = True
-
-    def either(eng, o, src, scale=1.0, bias=0.0):
-        i = len(ops)
-
-        def fn():
-            if ops[i]["eng"] == "scalar":
-                if bias == 0.0:
-                    return sq.activation(ap(o), ap(src), F.Copy)
-                return sq.activation(ap(o), ap(src), F.Identity, bias=bias, scale=scale)
-            if bias == 0.0:
-                return vq.tensor_copy(ap(o), ap(src))
-            return vq.tensor_scalar(ap(o), ap(src), scale, bias, A.mult, A.add)
-        add(eng, fn, [src], [o], vc(o[2] - o[1], 1.0))
-        ops[i]["flex"] = True
+    def gat(o, win, off, first="s", scale=1.0):
+        nel = o[2] - o[1]
+        s = ("scalar", ons(lambda: sq.activation(ap(o), ind(win, off), F.Copy, scale=scale), nel, "g"))
+        v = ("vector", onv(lambda: vq.tensor_scalar(ap(o), ind(win, off), scale, None, A.mult), nel, 1.0, "g"))
+        return add(dict([s, v] if first == "s" else [v, s]), [win, off], [o])
 
     def gtt(o, win, off, b, op):
-        add("vector", lambda: vq.tensor_tensor(ap(o), ind(win, off), ap(b), op), [win, off, b], [o], vc(o[2] - o[1], GA))
-        ops[-1]["gather"] = True
+        return add({"vector": onv(lambda: vq.tensor_tensor(ap(o), ind(win, off), ap(b), op), o[2] - o[1], 1.0, "g")},
+                   [win, off, b], [o])
+
+    def either(o, src, scale=1.0, bias=0.0):
+        nel = o[2] - o[1]
+        if bias == 0.0:
+            s = lambda: sq.activation(ap(o), ap(src), F.Copy, scale=scale)
+            v = lambda: vq.tensor_scalar(ap(o), ap(src), scale, None, A.mult)
+        else:
+            s = lambda: sq.activation(ap(o), ap(src), F.Identity, bias=bias, scale=scale)
+            v = lambda: vq.tensor_scalar(ap(o), ap(src), scale, bias, A.mult, A.add)
+        return add({"scalar": ons(s, nel), "vector": onv(v, nel, 0.5 if two(o, src) else 1.0)}, [src], [o])
+
+    def copy3(o, src, step=1):
+        nel = o[2] - o[1]
+        return add({"g": ong(lambda: g.affine_select(ap(o), ap(src, step), [[0, nel]], A.is_ge, 0.0, 0, 0), nel),
+                    "scalar": ons(lambda: sq.activation(ap(o), ap(src, step), F.Copy), nel),
+                    "vector": onv(lambda: vq.tensor_copy(ap(o), ap(src, step)), nel)}, [src], [o])
 
     def mset(o, val, step=1):
-        return add("vector", lambda: vq.memset(T[o[0]][:, o[1]:o[2]:step], val), [], [o],
-                   vc((o[2] - o[1]) // step, 0.5 if two(o) else 1.0))
+        return add({"vector": onv(lambda: vq.memset(ap(o, step), val), (o[2] - o[1]) // step, 0.5 if two(o) else 1.0)}, [], [o])
+
+    def gc(fn, r, w, nel):
+        return add({"g": ong(fn, nel)}, r, w)
 
     def mat(kind, name):
         k = {"F": MF, "B": MB, "H": MH}[kind].index(name)
         return ("MT" + kind, 128 * k, 128 * k + 128)
 
-    def mm(groups):
-        r, w, cost = [], [], 0.03
+    def mm(groups, late=None, begin=True, close=True, hold=None):
+        r, w, cyc = [], [hold] if hold else [], 0
         for o, terms in groups:
             w.append(o)
             for l, x, st in terms:
                 r += [l, x]
-                cost += max(64, o[2] - o[1]) * PC * (4 if SCRATCH[x[0]][2] == f32 else 1)
+                cyc += max(64, o[2] - o[1]) * (4 if SCRATCH[x[0]][2] == f32 else 1)
+        if late:
+            r += list(late[1][:2])
 
         def fn():
             last = None
             for o, terms in groups:
+                if late and ops[late[0]]["eng"] == "scalar":
+                    terms = terms + [late[1]]
                 for k, (l, x, st) in enumerate(terms):
-                    last = pq.matmul(ap(o), ap(l), T[x[0]][:, x[1]:x[2]:st], k == 0, k == len(terms) - 1)
+                    last = pq.matmul(ap(o), ap(l), ap(x, st), begin and k == 0, close and k == len(terms) - 1)
             return last
-        return add("tensor", fn, r, w, cost)
+        return add({"tensor": (fn, 0.05, cyc, "p")}, r, w)
 
-    def tolist(o, src, more=()):
-        terms = [(("VI", 128 * i, 128 * i + 128), (src[0], src[1] + i, src[2]), 16) for i in range(16)]
-        return mm([(o, terms + list(more))])
+    def steps(groups, apart=False):
+        nt = len(groups[0][1])
+        for k in range(nt):
+            for part in ([[x] for x in groups] if apart else [groups]):
+                mm([(o, terms[k:k + 1]) for o, terms in part], None, k == 0, k == nt - 1)
 
-    def dma(q, pairs, r, w, nbytes, accum=False):
+    def tolist(o, src, more=(), late=None):
+        terms = [(("VI", 16 - i, 144 - i), (src[0], src[1] + i, src[2]), 16) for i in range(16)]
+        return mm([(o, terms + list(more))], late)
+
+    def dma(q, pairs, r, w, nbytes, accum=0):
         eng = {"sync": g.sync, "scalar": g.scalar, "g": g}[q]
 
         def fn(sem):
             for o, i in pairs():
-                if accum:
+                if accum > 1:
+                    eng.dma_start(o, i, accum_op=A.add, max_dma_last_dim=accum).then_inc(sem, 16)
+                elif accum:
                     eng.dma_start(o, i, accum_op=A.add).then_inc(sem, 16)
                 else:
                     eng.dma_start(o, i).then_inc(sem, 16)
         cnt = len(pairs())
-        return add(q, fn, r, w, (1.0 if q == "g" else 0.1) * cnt, 2.0 + nbytes * (2 if accum else 1) / 500e3, "dma", cnt)
+        return add({q: (fn, 0.0 if q == "g" else 0.1 * cnt, cnt if q == "g" else 0, "d")}, r, w, "dma", cnt,
+                   nbytes * (2 if accum else 1))
 
     narr = [0]
 
@@ -203,7 +225,7 @@ def build(g, core, T, topo):
                 tr.append(RemoteDMATransfer(dst_ids=[DstId(rid=rid, pnc=pid)], dma_engine_mask=m,
                                             remote_sem=T.sem["arr%d" % k], src=ap(s), dst=ap(l)))
             g.remote_dma_fused(tr, local_sem=T.sem.sent)
-        i = add("g", fn, [s for _, s, _ in items], [l for _, _, l in items], 1.0, 3.0 if k else 4.5, "net", per * len(items))
+        i = add({"g": (fn, 1.0 if k else 2.5, 0, "c")}, [s for _, s, _ in items], [l for _, _, l in items], "net", per * len(items))
         ops[i]["sem"] = "arr%d" % k
         return i
 
@@ -211,25 +233,14 @@ def build(g, core, T, topo):
         k = US.index(name) * K
         return ("U", k + a, k + b)
 
-    def gc(fn, r, w, nel):
-        return add("g", fn, r, w, 0.15 + 2 * nel * CY)
-
-    def turned(o, i, turn, way):
-        if not turn:
-            return [(o[:, :], i)]
-        if way > 0:
-            return [(o[16:128, :], i[0:112, :]), (o[0:16, :], i[112:128, :])]
-        return [(o[0:112, :], i[16:128, :]), (o[112:128, :], i[0:16, :])]
-
-    def rows(t, a, b, c0, c1):
-        return t[a:b, c0:c1]
-
     def tpairs(ot, oc, it, ic, turn, way):
+        def rows(t, a, b, c):
+            return t[a:b, c[0]:c[1]]
         if not turn:
-            return [(rows(ot, 0, 128, *oc), rows(it, 0, 128, *ic))]
+            return [(rows(ot, 0, 128, oc), rows(it, 0, 128, ic))]
         if way > 0:
-            return [(rows(ot, 16, 128, *oc), rows(it, 0, 112, *ic)), (rows(ot, 0, 16, *oc), rows(it, 112, 128, *ic))]
-        return [(rows(ot, 0, 112, *oc), rows(it, 16, 128, *ic)), (rows(ot, 112, 128, *oc), rows(it, 0, 16, *ic))]
+            return [(rows(ot, 16, 128, oc), rows(it, 0, 112, ic)), (rows(ot, 0, 16, oc), rows(it, 112, 128, ic))]
+        return [(rows(ot, 0, 112, oc), rows(it, 16, 128, ic)), (rows(ot, 112, 128, oc), rows(it, 0, 16, ic))]
 
     dma("sync", lambda: tpairs(T.SXB, (0, 256), T.x0, (0, H), turn_l, -1) + tpairs(T.SXB, (256, 512), T.x0, (V - H, V), turn_r, 1),
         [], [("SXB", 0, 512)], 128 * 1024)
@@ -240,77 +251,80 @@ def build(g, core, T, topo):
     send([(left, ("SXB", 0, 256), ("XB", O1, O1 + H)), (right, ("SXB", 256, 512), ("XB", PAD, O0)),
           (right, ("SI", 0, 128), ("GI", 0, 128))])
 
+    def kf(j):
+        return ("KF", j, j + 1)
+    ONF, If = ("ONF", 0, 128), mat("F", "I")
+    ONE, NEG, SEV, WPC = (("CB", j * K, j * K + K) for j in range(4))
     gc(lambda: g.iota(T.KI[:, 0:2], [[0, 2]], 0, 1), [], [("KI", 0, 2)], 2)
+    mset(ONF, 1.0)
+    gc(lambda: g.affine_select(ap(If), ap(ONF), [[-1, 128]], A.is_equal, 0.0, 0, 1), [ONF], [If], 128)
     gc(lambda: g.iota(T.IO[:, :], [[16, CW]], 0, 0, allow_small_or_imprecise_dtypes=True), [], [("IO", 0, CW)], CW)
-    mset(("ONF", 0, K), 1.0)
-    mset(("ONB", 0, K), 1.0)
-    If = mat("F", "I")
-    gc(lambda: g.affine_select(ap(If), T.ONF[:, 0:128], [[-1, 128]], A.is_equal, 0.0, 0, 1), [("ONF", 0, 128)], [If], 128)
     gc(lambda: g.iota(T.RW[:, :], [[1, O0]], -O0 // 2, 0, allow_small_or_imprecise_dtypes=True), [], [("RW", 0, O0)], O0)
+    for c, val in ((ONE, 1.0), (NEG, -1.0), (SEV, 7.0), (WPC, float(WP))):
+        mset(c, val)
     ts(("KI", 2, 3), ("KI", 0, 1), 15, None, A.bitwise_and)
-    ts(("KI", 3, 4), ("KI", 0, 1), 4, None, A.arith_shift_right)
+    ts(("KI", 3, 4), ("KI", 0, 1), 1, None, A.bitwise_and)
     cp(("KF", 0, 2), ("KI", 2, 4))
-    ts(("KF", 2, 3), ("KF", 0, 1), 0.0, None, A.is_equal)
-    ts(("KF", 3, 4), ("KF", 0, 1), 1.0, float(O0 // 2), A.is_equal, A.mult)
-    ts(("IO", 0, CW), ("IO", 0, CW), T.KF[:, 0:1], None, A.add, extra=[("KF", 0, 1)])
-    for b in ("XB",):
-        mset((b, 0, PAD), FAR)
-        mset((b, WP - PAD, WP), FAR)
-    for o in (0, WP):
-        mset(("XF", o, o + PAD), FAR)
-        mset(("XF", o + WP - PAD, o + WP), FAR)
-
-    def sub(r, a, b):
-        return (r[0], r[1] + a, r[1] + b)
+    ts(kf(2), kf(0), 0.0, None, A.is_equal)
+    ts(kf(3), kf(0), 1.0, float(O0 // 2), A.is_equal, A.mult)
+    ts(kf(4), kf(1), -1.0, UQ * ZS, A.add, A.mult)
+    ts(kf(5), kf(1), -UL * ZS, None, A.mult)
+    ts(kf(6), kf(0), -LC - 1.0, ap(kf(5)), A.add, A.mult, extra=[kf(5)])
+    ts(kf(7), kf(0), -LC, ap(kf(5)), A.add, A.mult, extra=[kf(5)])
+    for j in range(2):
+        r0 = O0 // 2 + C0 - int(QC)
+        ts(("PV", j * K, j * K + K), ("RW", r0, r0 + K), ap(kf(4)), ap(kf(6 + j)), A.mult, A.add, extra=[kf(4), kf(6 + j)])
+    ts(("IO", 0, CW), ("IO", 0, CW), ap(kf(0)), None, A.add, extra=[kf(0)])
+    for b, o in (("XB", 0), ("XF", 0), ("XF", WP)):
+        mset((b, o, o + PAD), FAR)
+        mset((b, o + WP - PAD, o + WP), FAR)
 
     def scaled(o, c, turn=False, way=0):
         if not way:
-            act(o, If, F.Copy, scale=c)
+            either(o, If, c)
             return
         a, b = (16, 112) if way > 0 else (112, 16)
-        act(sub(o, a, 128), sub(If, 0, b) if turn else sub(If, a, 128), F.Copy, scale=c)
-        act(sub(o, 0, a), sub(If, b, 128) if turn else sub(If, 0, a), F.Copy, scale=c)
+        either(sub(o, a, 128), sub(If, 0, b) if turn else sub(If, a, 128), c)
+        either(sub(o, 0, a), sub(If, b, 128) if turn else sub(If, 0, a), c)
 
     def strided(o, o0, i0):
-        return add("vector", lambda: vq.tensor_copy(T[o[0]][:, o[1] + o0:o[2]:16], T[If[0]][:, If[1] + i0:If[2]:16]),
-                   [If], [o], vc(8, 1))
-    m = mat("F", "S1p"); cp(sub(m, 1, 128), sub(If, 0, 127)); mset(m, 0.0, 16)
-    m = mat("F", "S2p"); mset(m, 0.0); strided(m, 0, 15)
-    scaled(mat("F", "nI"), -1.0)
-    for nm, c in (("I", 1.0), ("I2", 2.0), ("nI2", -2.0), ("nI", -1.0), ("I3712", float(WP))):
-        scaled(mat("B", nm), c)
-    mset(("VI", 0, 2048), 0.0)
-    for q in range(8):
-        add("vector", lambda q=q: vq.tensor_scalar(T.VI[:, 16 * q:16 * q + 129 * 15 + 1:129], T.ONF[:, 0:16], T.KF[:, 1:2], float(q), A.mult, A.is_equal),
-            [("ONF", 0, 16), ("KF", 1, 2)], [("VI", 0, 2048)], vc(16, 1))
-        ops[-1]["par"] = "vi"
-    m = mat("F", "S1m"); cp(sub(m, 0, 127), sub(If, 1, 128)); mset(sub(m, 15, 128), 0.0, 16)
-    m = mat("F", "S2m"); mset(m, 0.0); strided(m, 15, 0)
-    scaled(mat("F", "I232"), float(CW))
-    scaled(mat("F", "RL"), 1.0, turn_l, -1)
-    scaled(mat("F", "RR"), 1.0, turn_r, 1)
-    scaled(mat("H", "I"), 1.0)
-    scaled(mat("H", "nI3712"), -float(WP))
-    kinds = ["B", "F"] + (["H"] if HALF else [])
-    for kd in kinds:
-        scaled(mat(kd, "P9"), 1.125); scaled(mat(kd, "N1"), -0.125)
-        if kd == "F" and HALF:
-            continue
-        scaled(mat(kd, "P9L"), 1.125, turn_l, -1); scaled(mat(kd, "N1L"), -0.125, turn_l, -1)
-        scaled(mat(kd, "P9R"), 1.125, turn_r, 1); scaled(mat(kd, "N1R"), -0.125, turn_r, 1)
-    for nm, c in (("nI", -1.0), ("I2", 2.0), ("nI2", -2.0)):
-        scaled(mat("H", nm), c)
-    scaled(mat("F", "I2"), 2.0)
-    scaled(mat("F", "nI2"), -2.0)
-    scaled(mat("B", "I7"), 7.0)
-    for b in ("TR", "TL"):
-        gc(lambda b=b: g.iota(T[b][:, :], [[0, WP]], 0, 0, allow_small_or_imprecise_dtypes=True), [], [(b, 0, WP)], WP)
+        return add({"vector": onv(lambda: vq.tensor_copy(ap(sub(o, o0, 128), 16), ap(sub(If, i0, 128), 16)), 8)}, [If], [o])
+    for s1, s2, d1, a, b in (("S1p", "S2p", "D1p", 1, 0), ("S1m", "S2m", "D1m", 0, 1)):
+        m = mat("F", s1)
+        cp(sub(m, a, 128 - b), sub(If, b, 128 - a))
+        mset(sub(m, 15 * b, 128), 0.0, 16)
+        tt(mat("F", d1), m, If, A.subtract)
+        m = mat("F", s2)
+        mset(m, 0.0)
+        strided(m, 15 * b, 15 * a)
+    mset(("VI", 0, 144), 0.0)
+    gc(lambda: g.affine_select(T.VI[:, 16:144:16], T.ONF[:, 0:8], [[-16, 8]], A.is_ge, 0.0, 0, 1), [ONF], [("VI", 0, 144)], 8)
+    gc(lambda: g.affine_select(T.VI[:, 16:144:16], T.VI[:, 16:144:16], [[16, 8]], A.is_ge, 0.0, 15, -1), [], [("VI", 0, 144)], 8)
+    mset(("VP", 0, 144), 0.0)
+    mset(("KF", 8, 16), ZS)
+    for j, s in enumerate((HI, LO)):
+        gc(lambda j=j, s=s: g.affine_select(T.VP[:, 16 + j:144:16], T.KF[:, 8:16], [[-s.step, 8]], A.is_equal, 0.0, -s.start, 1),
+           [("KF", 8, 16)], [("VP", 0, 144)], 8)
+    mset(("PR", 0, 136), 0.0)
+    add({"vector": onv(lambda: vq.tensor_tensor(T.PR[:, 1:129:2], ap(If, 2), ap(sub(If, 1, 128), 2), A.add), 64, 2.0)},
+        [If], [("PR", 0, 136)])
+    either(("PR", 0, 136), ("PR", 0, 136), 8192.0)
+    for kd, nm, c in (("H", "I", 1.0), ("H", "Ih", 0.5), ("B", "I", 1.0), ("B", "nI", -1.0), ("F", "ITW", float(TW)),
+                      ("H", "nTN", -float(TN)), ("H", "n16", -16.0), ("H", "N1", -0.125), ("B", "P9", 1.125),
+                      ("H", "nI", -1.0), ("H", "P9", 1.125), ("F", "nI", -1.0), ("F", "Ih", 0.5), ("F", "P9", 1.125),
+                      ("F", "N1", -0.125)):
+        if nm != "Ih" or kd != "F" or "p" in OPT["form"][2]:
+            scaled(mat(kd, nm), c)
+    for kd, nm, c in (("F", "R", 1.0), ("B", "P9", 1.125), ("H", "P9", 1.125), ("H", "N1", -0.125)):
+        scaled(mat(kd, nm + "L"), c, turn_l, -1)
+        scaled(mat(kd, nm + "R"), c, turn_r, 1)
+    for a in range(0, TN, TN // 4):
+        add({"g": ong(lambda a=a: g.iota(T.TR[:, a:a + TN // 4], [[0, TN // 4]], 0, 0, allow_small_or_imprecise_dtypes=True), TN // 4),
+             "vector": onv(lambda a=a: vq.memset(T.TR[:, a:a + TN // 4], 0.0), TN // 4, 0.5)}, [], [("TR", a, a + TN // 4)])
     for b in ("A2", "A4"):
-        ts((b, 0, O0), ("RW", 0, O0), T.KF[:, 2:3], T.KF[:, 3:4], A.mult, A.add, extra=[("KF", 2, 4)])
-    mset(("HR", 0, 2 * CW), 0.0)
-    mset(("HL", 0, 2 * CW), 0.0)
-    cp(("HA", 0, CW), ("IO", 0, CW))
-    tt(("HA", CW, 2 * CW), ("IO", 0, CW), ("HA", 0, CW), A.subtract)
+        ts((b, 0, O0), ("RW", 0, O0), ap(kf(2)), ap(kf(3)), A.mult, A.add, extra=[("KF", 2, 4)])
+    cp(("HA", 0, 16), ("IO", C0 - 16, C0))
+    tt(("HA", TW, TW + 16), ("IO", C0 - 16, C0), ("HA", 0, 16), A.subtract)
     IOo = ("IO", C0, C1)
 
     def nl(k, t, a, b):
@@ -318,7 +332,7 @@ def build(g, core, T, topo):
 
     for j, k in enumerate("RL"):
         ts(nl(k, 0, C0, C1), ("LI", j * K, j * K + K), float(PAD), None, A.add)
-        cp(u("e" + k), nl(k, 0, C0, C1))
+        ts(u("e" + k), ("LI", j * K, j * K + K), float(PAD), None, A.add)
     ts(nl("L", 0, C0 - 1, C0), ("GI", 63, 64), float(PAD - V), None, A.add)
     ts(nl("R", 0, C0 - 1, C0), ("GI", 127, 128), float(PAD - V), None, A.add)
 
@@ -326,39 +340,35 @@ def build(g, core, T, topo):
 
     def cands(t):
         d = 1 if t % 2 == 0 else -1
-        s1, s2 = (mat("F", "S1p"), mat("F", "S2p")) if d > 0 else (mat("F", "S1m"), mat("F", "S2m"))
+        sfx = "p" if d > 0 else "m"
         for k in "RL":
-            sh = [(s1, nl(k, t, C0, C1), 1), (s2, nl(k, t, C0 - d, C1 - d), 1)]
-            mm([((bank[k], 0, K), sh)])
+            far = (mat("F", "S2" + sfx), nl(k, t, C0 - d, C1 - d), 1)
+            mm([((bank[k], 0, K), [(mat("F", "S1" + sfx), nl(k, t, C0, C1), 1), far])])
             if k == "R":
                 ts(u("cR"), (bank[k], 0, K), float(d), float(WP - PAD), A.add, A.min)
             else:
                 ts(u("cL"), (bank[k], 0, K), float(d), float(PAD - 1), A.add, A.max)
-            mm([((bank[k], K, 2 * K), sh + [(mat("F", "nI"), nl(k, t, C0, C1), 1),
-                                            (mat("F", "I" if d > 0 else "nI"), ("ONF", 0, K), 1)])])
+            mm([((bank[k], K, 2 * K), [(mat("F", "D1" + sfx), nl(k, t, C0, C1), 1), far, (mat("B", "I"), ONE if d > 0 else NEG, 1)])])
 
-    def table(tab, h):
-        def pairs():
-            out = []
-            for half in range(2):
-                p = 64 * half
-                out.append((T[tab][p:p + 61:20, :], T[h][p:p + 64, 0:CW]))
-                out.append((T[tab][p + 12:p + 49:12, :], T[h][p:p + 64, CW:2 * CW]))
-            return out
-        dma("sync", pairs, [(h, 0, 2 * CW)], [(tab, 0, WP)], 128 * 1000)
+    def table(h):
+        dma("sync", lambda: [(T.TR[HI, :], T[h][:, 0:TW]), (T.TR[LO, :], T[h][:, TW:2 * TW])], [(h, 0, 2 * TW)], [("TR", 0, TN)], 128 * 1000)
 
-    def tabpos(o, src, qm, ps):
-        either("scalar", qm, src, 0.0625, 1024.0 - 0.46875)
-        mm([(ps, [(mat("F", "I232"), src, 1), (mat("H", "nI3712"), qm, 1), (mat("H", "I"), qm, 1)])])
-        ts(o, ps, float((WP - 1) * 1024), None, A.add)
+    def quot(qm, src):
+        either(qm, src, 0.0625, QO - 0.46875)
 
-    def hilo(h, src, a, b, e, ps=None):
-        either(ENG[e], (h, a, b), src)
+    def tabpos(o, src, qm, ps, first):
+        quot(qm, src)
+        mm([(ps, [(mat("F", "ITW"), src, 1), (mat("H", "nTN"), qm, 1), (mat("H", "I"), qm, 1)])])
+        ts(o, ps, (TN - 1) * QO - first, None, A.add)
+
+    def hilo(h, src, a, b, ps=None):
+        either((h, a, b), src)
         if ps:
-            mm([((ps, 0, b - a), [(mat("F", "I"), src, 1), (mat("B", "nI"), (h, a, b), 1)])])
-            either(ENG[e], (h, CW + a, CW + b), (ps, 0, b - a))
+            ps = (ps[0], ps[1], ps[1] + b - a)
+            mm([(ps, [(If, src, 1), (mat("B", "nI"), (h, a, b), 1)])])
+            either((h, TW + a, TW + b), ps)
         else:
-            tt((h, CW + a, CW + b), src, (h, a, b), A.subtract)
+            tt((h, TW + a, TW + b), src, (h, a, b), A.subtract)
 
     nse = [0]
 
@@ -375,7 +385,10 @@ def build(g, core, T, topo):
                 items.append((right, se, nl(k, t + 1, C0 - 16, C0)))
         mm(gr)
         for (ps, _), (k, way), it in zip(gr, what, items):
-            either("scalar", it[1], ps, 1.0, -float(way * V))
+            if (k, way) == ("L", -1):
+                ts(it[1], ps, float(V), TOP, A.add, A.min)
+            else:
+                either(it[1], ps, 1.0, -float(way * V))
         send(items)
 
     qn = [0]
@@ -387,14 +400,18 @@ def build(g, core, T, topo):
 
     def eslot():
         en[0] += 1
-        return "E0" if en[0] % 2 else "E1"
+        return 512 * (en[0] % 2)
 
     XS = [("XB", 0), ("XF", WP), ("XF", 0)]
     cands(0)
+    pend = []
     for t in range(RO):
         xb, xo = XS[t]
         kd = KD[t]
+        kg = "F" if kd == "F" else "H"
         win = (xb, xo, xo + WP)
+        last = t == RO - 1
+        order = [(x[0], int(x[1])) for x in OPT["order"][t].split()]
 
         def xown(a, b):
             return (xb, xo + O0 + a, xo + O0 + b)
@@ -404,159 +421,186 @@ def build(g, core, T, topo):
 
         def xc(a, b):
             return ("XH", a, b) if kd == "H" else (xb, xo + WP + O0 + a, xo + WP + O0 + b)
-        gen, ppn, wb = {"B": ("GE", "PP", "GE"), "H": ("GH", "PH", "GH"), "F": ("FA", "FB", "DW")}[kd]
-
-        def ring(nm, a, b):
-            return (nm, a % 2048, a % 2048 + b - a) if nm in ("FA", "FB") else (nm, a, b)
 
         def ge(a, b):
-            return ring(gen, a, b)
+            return ("FA" if kd == "F" else "GH", a, b)
 
         def pp(a, b):
-            return ring(ppn, a, b)
-        last = t == RO - 1
-        for c in range(3):
+            return ("FB" if kd == "F" else "PH", a, b)
+        for c in (2, 0, 1):
             a, b = 1024 * c, 1024 * c + 1024
             if kd == "H":
-                either("scalar", xc(a, b), xown(a, b))
+                copy3(xc(a, a + 512), xown(a, a + 512))
+                copy3(xc(a + 512, b), xown(a + 512, b))
             elif t:
                 dma("sync", lambda o=xc(a, b), i=xown(a, b): [(ap(o), ap(i))], [xown(a, b)], [xc(a, b)], 512 * 1024)
         if t == 0:
             dma("sync", lambda o=xc(0, V): [(ap(o), T.x0[:, :])], [], [xc(0, V)], 128 * 6144)
-        dma("g" if xb == "XB" else "sync",
-            lambda xb=xb, xo=xo: [(T.MA[:, 0:O0], T[xb][:, xo:xo + O0]), (T.MB[:, 0:O0], T[xb][:, xo:xo + O0])],
-            [(xb, xo, xo + O0)], [("MA", 0, O0), ("MB", 0, O0)], 128 * 2560)
         dma("sync", lambda xb=xb, xo=xo: [(T[xb][:, xo + WP:xo + WP + O0], T[xb][:, xo:xo + O0])],
             [(xb, xo, xo + O0)], [(xb, xo + WP, xo + WP + O0)], 128 * 1280)
-        for j, k in enumerate("RL"):
+        for i in range(16):
+            copy3(("XP", TW * i, TW * i + TW), (xb, xo + O0 + i, xo + O1 + H), 16)
+        main = {"R": ("R", 1), "L": ("L", -1)}
+        extra = [] if last else [("L", 1)] if t % 2 else [("R", -1)]
+        done = []
+        for nc, (k, c) in enumerate(order):
             bk = bank[k]
-            for nc, c in enumerate((2, 0, 1) if k == "R" else (0, 1, 2)):
+            j = "RL".index(k)
+            jq = j * TW
+            if True:
                 a, b = 1024 * c, 1024 * c + 1024
                 ue, uc = u("e" + k, 64 * c, 64 * c + 64), u("c" + k, 64 * c, 64 * c + 64)
-                q = qslot()
-                form = OPT["form"][t][3 * j + c]
-                r0 = 1024 * (3 * j + nc) if kd == "F" else a
+                q = OPT["slots"][nc % len(OPT["slots"])]
+                form = OPT["form"][t][nc]
+                r0 = 1024 * (nc % 3)
                 g1, p1 = ge(r0, r0 + 1024), pp(r0, r0 + 1024)
-                more = []
+                ne = ("NE", 1024 * (nc % 4), 1024 * (nc % 4) + 1024)
+                late = None
                 if form == "a":
                     gtt(g1, win, uc, xc(a, b), A.subtract)
                     gtt(p1, win, ue, xc(a, b), A.subtract)
                     act((q, 0, 1024), g1, F.Abs)
                     act(p1, p1, F.Abs)
-                    tt(("NE", a, b), (q, 0, 1024), p1, A.is_lt)
+                    tt(ne, (q, 0, 1024), p1, A.is_lt)
                 elif form == "c":
-                    gat("scalar", g1, win, uc)
+                    gat(g1, win, uc)
                     gtt(p1, win, ue, xc(a, b), A.subtract)
-                    mm([((q, s, s + 512), [(mat(kd, "I"), sub(g1, s, s + 512), 1), (mat(kd, "nI"), xpe(a + s, a + s + 512), 1)]) for s in (0, 512)])
+                    steps([((q, s, s + 512), [(mat(kd, "nI"), xpe(a + s, a + s + 512), 1), (mat(kg, "I"), sub(g1, s, s + 512), 1)]) for s in (0, 512)], True)
                     act((q, 0, 1024), (q, 0, 1024), F.Abs)
                     act(p1, p1, F.Abs)
-                    tt(("NE", a, b), (q, 0, 1024), p1, A.is_lt)
+                    tt(ne, (q, 0, 1024), p1, A.is_lt)
                 else:
-                    gat("scalar", g1, win, ue)
+                    gat(g1, win, ue)
                     gtt(p1, win, uc, g1, A.subtract)
-                    mm([((q, s, s + 512), [(mat(kd, "I2"), sub(g1, s, s + 512), 1), (mat(kd, "nI2"), xpe(a + s, a + s + 512), 1),
-                                           (mat(kd, "I"), sub(p1, s, s + 512), 1)]) for s in (0, 512)])
-                    tt(("NE", a, b), (q, 0, 1024), p1, A.mult)
-                    if form == "v":
-                        ts(("NE", a, b), ("NE", a, b), 0.0, None, A.is_lt)
-                    else:
-                        act(("NE", a, b), ("NE", a, b), F.Sign, scale=-1.0, bias=-2.0 ** -26)
-                        more = [(mat("B", "I7"), ("ONB", 0, 64), 1)]
-                tolist((bk, 64 * c, 64 * c + 64), ("NE", a, b), more)
-                if (k, c) not in GROUPS:
+                    steps([((q, s, s + 512), [(mat(kd, "nI"), xpe(a + s, a + s + 512), 1), (mat(kg, "I"), sub(g1, s, s + 512), 1),
+                                              (mat(kg, "Ih"), sub(p1, s, s + 512), 1)]) for s in (0, 512)], kd == "F")
+                    tt(ne, (q, 0, 1024), p1, A.mult)
+                    i = add({"scalar": ons(lambda ne=ne: sq.activation(ap(ne), ap(ne), F.Sign, bias=-2.0 ** -27, scale=-1.0), 1024),
+                             "vector": onv(lambda ne=ne: vq.tensor_scalar(ap(ne), ap(ne), 0.0, None, A.is_lt), 1024, 0.5)}, [ne], [ne])
+                    late = (i, (mat("B", "I"), sub(SEV, 0, 64), 1))
+                tolist((bk, 64 * c, 64 * c + 64), ne, late=late)
+                if (k, c) not in OPT["groups"][t]:
                     continue
-                ca, cb = GROUPS[k, c]
+                ca, cb = OPT["groups"][t][k, c]
                 tv = ("TT", j * K + ca, j * K + cb)
                 new = nl(k, t + 1, C0 + ca, C0 + cb)
                 ts(tv, (bk, ca, cb), 8.5, None, A.is_ge)
                 tt((bk, K + ca, K + cb), (bk, K + ca, K + cb), tv, A.mult)
                 tt(new, (bk, K + ca, K + cb), nl(k, t, C0 + ca, C0 + cb), A.add)
-                if k == "R" and cb == K:
-                    edges(t, [("R", 1)], bk)
-                tabpos(u("t" + k, ca, cb), new, ("QM", j * K + ca, j * K + cb), (bk, ca, cb))
-                if k == "R" or not last:
-                    cp(u("e" + k, ca, cb), new)
-            if k == "L":
-                edges(t, [("L", -1)] + ([] if last else [("L", 1)] if t % 2 else [("R", -1)]), bk)
-            a, b = (C0 - 16, C1) if k == "R" else (C0, C1 + 16)
-            hilo("H" + k, nl(k, t + 1, a, b), a, b, OPT["hi"][t][j], bk if LOPE[j] else None)
-            table("T" + k, "H" + k)
+                done += [(k, -1)] * (ca == 0) + [(k, 1)] * (cb == K)
+                if main.get(k) in done:
+                    now = [main.pop(k)] + [e for e in extra if e in done]
+                    extra = [e for e in extra if e not in now]
+                    edges(t, now, bk)
+                tabpos(u("t" + k, ca, cb), new, ("QM", jq + ca, jq + cb), (bk, ca, cb), C0 if k == "R" else C0 - 16)
+            if k in [x[0] for x in order[nc + 1:]]:
+                continue
+            if not last:
+                pend.append(lambda k=k, t=t: cp(u("e" + k), nl(k, t + 1, C0, C1)))
+            if k == "R":
+                hilo("HR", nl(k, t + 1, C0 - 16, C1), 0, TW, (bk, 0) if OPT["lope"][0] else None)
+                table("HR")
+            else:
+                qm = ("QM", jq, jq + TW)
+                quot(sub(qm, K, TW), nl(k, t + 1, C1, C1 + 16))
+                either(("HL", 0, TW), qm, UQ, -(QO + QC) * UQ)
+                mm([((bk, 0, TW), [(If, nl(k, t + 1, C0, C1 + 16), 1), (mat("H", "n16"), qm, 1)])])
+                either(("HL", TW, 2 * TW), (bk, 0, TW), UL, (16 * QO - LC) * UL)
+                for j, s in enumerate((HI, LO)):
+                    i = dma("g", lambda j=j, s=s: [(T.XP[s, :], T.HL[:, j * TW:j * TW + TW])],
+                            [("HL", j * TW, j * TW + TW)], [("XP", 0, TN)], 128 * 1000, accum=4 * TW)
+                    ops[i]["beside"] = t
+        if extra:
+            edges(t, extra, bank[extra[0][0]])
+        def cut(name):
+            e = OPT[name][t]
+            return [(V // len(e) * h, V // len(e) * (h + 1), e[h]) for h in range(len(e))]
+
+        def mstep(src, lst, first, nxt, t=t, xc=xc):
+            w = V // OPT["mparts"][t]
+            for a in range(0, V, w):
+                b = a + w
+                gtt(("MP", a, b), (src[0], src[1], src[1] + O0 + b), u(lst, a // 16, b // 16), xc(a, b) if first else ("MP", a, b), A.max)
+                if nxt:
+                    dma("sync", lambda a=a, b=b: [(T[nxt][:, O0 + a:O0 + b], T.MP[:, a:b])], [("MP", a, b)], [(nxt, O0 + a, O0 + b)], 512 * (b - a))
+        for a, b, e in cut("rl"):
+            gat(("A4", O0 + a, O0 + b), ("TR", 0, TN), u("tL", a // 16, b // 16), e)
+            tolist(("LA", a // 16, b // 16), ("A4", O0 + a, O0 + b))
+            if b in OPT["a1ends"][t]:
+                ca, cb = ([0] + [x // 16 for x in OPT["a1ends"][t] if x < b])[-1], b // 16
+                ps, io, na = ("LA", ca, cb), ("IO", C0 + ca, C0 + cb), ("NA", ca, cb)
+                tt(ps, ps, io, A.not_equal)
+                tt(ps, ps, io, A.mult)
+                tt(na, ps, nl("L", t + 1, C0 + ca, C0 + cb), A.max)
+                hilo("HA", na, 16 + ca, 16 + cb, ("LA", ca) if OPT["lope"][1] else None)
+                if b == V:
+                    table("HA")
+                cp(u("a1", ca, cb), na)
+                tabpos(u("ta", ca, cb), na, ("QM", 2 * TW + ca, 2 * TW + cb), ps, C0 - 16)
+        for fn in pend:
+            fn()
+        dma("g" if xb == "XB" else "sync",
+            lambda xb=xb, xo=xo: [(T.MA[:, 0:O0], T[xb][:, xo:xo + O0]), (T.MB[:, 0:O0], T[xb][:, xo:xo + O0])],
+            [(xb, xo, xo + O0)], [("MA", 0, O0), ("MB", 0, O0)], 128 * 2560)
+        mstep((xb, xo), "a1", True, "MA")
+        nb = [0]
+
+        def lists(name, o, src, lst, more=None):
+            for a, b, e in cut(name):
+                ca, cb = a // 16, b // 16
+                nb[0] += 1
+                ps = ("LA" if nb[0] % 2 else "LB", 0, cb - ca)
+                gat((o, O0 + a, O0 + b), (src, 0, TN if src == "TR" else O0 + b), u(lst, ca, cb), e)
+                tolist(ps, (o, O0 + a, O0 + b), [(mat("B", "I"), sub(more, 0, cb - ca), 1)] if more else [])
+                yield ca, cb, ps
+        for ca, cb, ps in lists("a2", "A2", "TR", "ta"):
+            cp(u("a2", ca, cb), ps)
+            either(("HH", ca, cb), ps)
+        zb = "QE"
+        pend = []
         for c in range(3):
             a, b = 1024 * c, 1024 * c + 1024
-            ue = u("eR", 64 * c, 64 * c + 64)
-            if OPT["w"][t][c] == "s":
-                gat("scalar", (wb, a, b), win, ue)
-                for s in (a, a + 512):
-                    e = eslot()
-                    mm([((e, 0, 512), [(mat(kd, "I"), (wb, s, s + 512), 1), (mat(kd, "nI"), xpe(s, s + 512), 1)])])
-                    act(("DW", s, s + 512), (e, 0, 512), F.Abs)
+            ut = u("tR", 64 * c, 64 * c + 64)
+            fused = OPT["w"][t][c] == "v"
+            if fused:
+                gtt(("DW", a, b), ("XP", 0, TN), ut, xown(a, b), A.subtract)
             else:
-                gtt(("DW", a, b), win, ue, xc(a, b), A.subtract)
-                act(("DW", a, b), ("DW", a, b), F.Abs)
-        hv = [(s, s + V // PARTS[t]) for s in range(0, V, V // PARTS[t])]
-        pw = K // PARTS[t]
-
-        def eng(nm, h):
-            return ENG[OPT[nm][t][h]]
-
-        def mstep(src, lst, first, nxt):
-            for a, b in hv:
-                gtt(("MP", a, b), (src[0], src[1], src[1] + O0 + b), u(lst, a // 16, b // 16), xc(a, b) if first else ("MP", a, b), A.max)
-            if nxt:
-                for a, b in hv:
-                    dma("sync", lambda a=a, b=b: [(T[nxt][:, O0 + a:O0 + b], T.MP[:, a:b])], [("MP", a, b)], [(nxt, O0 + a, O0 + b)], 512 * (b - a))
-        for h, (a, b) in enumerate(hv):
-            gat(eng("rl", h), ("A4", O0 + a, O0 + b), ("TR", 0, WP), u("tL", a // 16, b // 16))
-            tolist(("LA", a // 16, b // 16), ("A4", O0 + a, O0 + b))
-        tt(("LA", 0, K), ("LA", 0, K), IOo, A.not_equal)
-        tt(("LA", 0, K), ("LA", 0, K), IOo, A.mult)
-        tt(("NA", 0, K), ("LA", 0, K), nl("L", t + 1, C0, C1), A.max)
-        hilo("HA", ("NA", 0, K), C0, C1, OPT["hi"][t][2], "LA" if LOPE[2] else None)
-        table("TR", "HA")
-        tabpos(u("ta"), ("NA", 0, K), ("QM", 2 * K, 3 * K), ("LA", 0, K))
-        cp(u("a1"), ("NA", 0, K))
-        for h, (a, b) in enumerate(hv):
-            gat(eng("lr", h), ("NE", a, b), ("TL", 0, WP), u("tR", a // 16, b // 16))
-        tolist(("LB", 0, K), ("NE", 0, V))
-        tt(("EN", 0, K), ("LB", 0, K), IOo, A.not_equal)
-        mstep((xb, xo), "a1", True, "MA")
-        for h, (a, b) in enumerate(hv):
-            ca, cb = a // 16, b // 16
-            ps = ("LB" if h % 2 else "LA", 0, pw)
-            gat(eng("a2", h), ("A2", O0 + a, O0 + b), ("TR", 0, WP), u("ta", ca, cb))
-            tolist(ps, ("A2", O0 + a, O0 + b))
-            cp(u("a2", ca, cb), ps)
-            tt(("HH", ca, cb), ps, ("EN", ca, cb), A.mult)
+                gat(("DW", a, b), ("XP", 0, TN), ut, "s", -1.0)
+            for j in range(2):
+                zo = (zb, j * K + 64 * c, j * K + 64 * c + 64)
+                terms = [(("VP", 16 - r, 144 - r), ("DW", a + r + j, b), 16) for r in range(0, 16, 2)]
+                terms.append((mat("B", "I" if fused else "nI"), ("PV", j * K + 64 * c, j * K + 64 * c + 64), 1))
+                mm([(zo, terms[:4])], None, True, False, (zb, 0, 512))
+                mm([(zo, terms[4:])], None, False, True, (zb, 0, 512))
+            if not fused:
+                dma("g", lambda a=a, b=b, i=xown(a, b): [(T.DW[:, a:b], ap(i))], [xown(a, b)], [("DW", a, b)], 512 * 1024, accum=1)
+            pend.append(lambda a=a, b=b: act(("DW", a, b), ("DW", a, b), F.Abs))
         mstep(("MA", 0), "a2", False, "MB")
-        for h, (a, b) in enumerate(hv):
-            ca, cb = a // 16, b // 16
-            ps = ("LB" if (h + PARTS[t]) % 2 else "LA", 0, pw)
-            gat(eng("a4", h), ("A4", O0 + a, O0 + b), ("A2", 0, O0 + b), u("a2", ca, cb))
-            tolist(ps, ("A4", O0 + a, O0 + b))
+        for ca, cb, ps in lists("a4", "A4", "A2", "a2"):
             cp(u("a4", ca, cb), ps)
             tt(("GO", ca, cb), ps, ("HH", ca, cb), A.is_lt)
-        mstep(("MB", 0), "a4", False, "MA")
-        for h, (a, b) in enumerate(hv):
-            ca, cb = a // 16, b // 16
-            ps = ("LB" if h % 2 else "LA", 0, pw)
-            gat(eng("a8", h), ("A2", O0 + a, O0 + b), ("A4", 0, O0 + b), u("a4", ca, cb))
-            tolist(ps, ("A2", O0 + a, O0 + b), [(mat("B", "I3712"), ("ONB", 0, pw), 1)])
+        cp(("LI", 0, 2 * K), (zb, 0, 2 * K))
+        tt(("FL", 0, 2 * K), (zb, 0, 2 * K), ("LI", 0, 2 * K), A.not_equal)
+        mm([((zb, 0, K), [(("PR", 1, 129), ("FL", 0, K), 1), (("PR", 0, 128), ("FL", K, 2 * K), 1)])])
+        tt((zb, 0, K), (zb, 0, K), ("GO", 0, K), A.mult)
+        tt(("GO", 0, K), (zb, 0, K), IOo, A.max)
+        for ca, cb, ps in lists("a8", "A2", "A4", "a4", WPC):
             ts(u("a8", ca, cb), ps, -float(WP), None, A.add)
-            tt(ps, ps, ("GO", ca, cb), A.mult)
-            tt(ps, ps, ("IO", C0 + ca, C0 + cb), A.max)
+            tt(ps, ps, ("GO", ca, cb), A.min)
             cp(u("s", ca, cb), ps)
+        mstep(("MB", 0), "a4", False, "MA")
         if not last:
             cands(t + 1)
-        for h, (a, b) in enumerate(hv):
-            gat(eng("x8", h), (xb, xo + WP + O0 + a, xo + WP + O0 + b), (xb, xo, xo + O0 + b), u("a8", a // 16, b // 16))
+        for a, b, e in cut("x8"):
+            gat((xb, xo + WP + O0 + a, xo + WP + O0 + b), (xb, xo, xo + O0 + b), u("a8", a // 16, b // 16), e)
         nxs = [0]
 
         def xs(a, b):
-            gat(eng("xs", nxs[0]), ge(a, b), (xb, xo, xo + WP + O0 + b), u("s", a // 16, b // 16))
+            gat(ge(a, b), (xb, xo, xo + WP + O0 + b), u("s", a // 16, b // 16), OPT["xs"][t][nxs[0]])
             nxs[0] += 1
 
         def zz(o, a, b, sfx):
-            return (o, [(mat(kd, "P9" + sfx), xpe(a, b), 1), (mat(kd, "N1" + sfx), ge(a, b), 1)])
+            return (o, [(mat(kd, "P9" + sfx), xpe(a, b), 1), (mat(kg, "N1" + sfx), ge(a, b), 1)])
         if not last:
             nb, no = XS[t + 1]
             xs(0, H)
@@ -568,30 +612,37 @@ def build(g, core, T, topo):
             send([(left, ("SXF", sx, sx + H), (nb, no + O1, no + O1 + H)), (right, ("SXF", sx + H, sx + 512), (nb, no + PAD, no + O0))])
             for a, b in ((H, 1024), (1024, 2048), (2048, V - H)):
                 xs(a, b)
-            mv = [(0, 1024), (1024, 2048), (2048, V)]
+            for a in (2048, 0, 1024):
+                q = qslot()
+                steps([zz((q, s - a, s - a + 512), s, s + 512, "") for s in (a, a + 512)])
+                ts((nb, no + O0 + a, no + O0 + a + 1024), (q, 0, 1024), 0.0, 4.0, A.max, A.min)
         else:
-            mv = [(0, 1024), (1024, 2048), (2048, 2560), (2560, V)]
-        for a, b in mv:
-            if last:
+            for a, b, q in ((0, 1024, "QA"), (1024, 2048, "QB"), (2048, 2560, "LA"), (2560, V, "LB")):
+                two_terms = [zz((q, s - a, s - a + 512), s, s + 512, "") for s in range(a, b, 512)]
+                for o, terms in two_terms:
+                    mm([(o, terms[:1])], close=False)
                 xs(a, b)
-            q = qslot()
-            mm([zz((q, s - a, s - a + 512), s, s + 512, "") for s in range(a, b, 512)])
-            if last:
+                for o, terms in two_terms:
+                    mm([(o, terms[1:])], begin=False)
                 ts(pp(a, b), (q, 0, b - a), 0.0, 4.0, A.max, A.min)
                 dma("sync", lambda a=a, b=b, i=pp(a, b): [(T.xe[:, a:b], ap(i))], [pp(a, b)], [], 512 * (b - a))
-            else:
-                ts((nb, no + O0 + a, no + O0 + b), (q, 0, b - a), 0.0, 4.0, A.max, A.min)
-        mstep(("MA", 0), "a8", False, None)
-        ends = [1536, V] if not last else [1024, 2048, 2560, V]
-        s0 = 0
-        for s in range(0, V, 512):
-            e = eslot()
-            act((e, 0, 512), ("DW", s, s + 512), F.Exp, scale=-1.0)
-            tt(("MP", s, s + 512), (e, 0, 512), ("MP", s, s + 512), A.mult)
-            if s + 512 in ends:
-                dma("g" if t else "sync", lambda a=s0, b=s + 512: [(T.ye[:, a:b], T.MP[:, a:b])], [("MP", s0, s + 512)],
-                    [("ye", s0, s + 512)], 512 * (s + 512 - s0), accum=t > 0)
-                s0 = s + 512
+        def grow(t=t, last=last, mstep=mstep):
+            mstep(("MA", 0), "a8", False, None)
+            w = 512 if last else 1024
+            ends = [1024, 2048, 2560, V] if last else [2048, V]
+            s0 = 0
+            for s in range(0, V, w):
+                e = sub(("QE", eslot(), 0), 0, w) if last else (qslot(), 0, w)
+                act(e, ("DW", s, s + w), F.Exp, scale=-1.0)
+                yb = "DW" if last else "FB"
+                tt((yb, s, s + w), e, ("MP", s, s + w), A.mult)
+                if s + w in ends:
+                    dma("g" if t else "sync", lambda a=s0, b=s + w, yb=yb: [(T.ye[:, a:b], T[yb][:, a:b])], [(yb, s0, s + w)],
+                        [("ye", s0, s + w)], 512 * (s + w - s0), accum=int(t > 0))
+                    s0 = s + w
+        pend.append(grow)
+    for fn in pend:
+        fn()
     return ops
 
 
@@ -603,16 +654,27 @@ def depends(ops):
         acc = [(r, False) for r in o["r"]] + [(w, True) for w in o["w"]]
         for (nm, a, b), wr in acc:
             for j, a2, b2, wr2 in seen.get(nm, ()):
-                if nm in PSUM and (ops[j]["eng"] != o["eng"] or o.get("flex") or ops[j].get("flex")):
-                    d.add(j)
-                elif (wr or wr2) and a < b2 and a2 < b:
-                    if not (o.get("par") and o.get("par") == ops[j].get("par")):
+                if nm in PSUM and (ops[j]["eng"] != o["eng"] or len(o["alts"]) > 1 or len(ops[j]["alts"]) > 1):
+                    if a // 512 <= (b2 - 1) // 512 and a2 // 512 <= (b - 1) // 512:
                         d.add(j)
+                elif (wr or wr2) and a < b2 and a2 < b and o.get("beside", -1) != ops[j].get("beside", -2):
+                    d.add(j)
         for (nm, a, b), wr in acc:
             seen.setdefault(nm, []).append((i, a, b, wr))
         d.discard(i)
         deps.append(d)
     return deps
+
+
+QUEUES = ["vector", "scalar", "tensor", "sync", "g"]
+
+
+def times(ops, speed):
+    f, ga, pe, hop, dm, net, gd = speed
+    per = {"c": CY * f, "g": CY * f * ga, "p": pe, "d": gd}
+    cost = [[o["alts"][e][1] + o["alts"][e][2] * per[o["alts"][e][3]] if e in o["alts"] else None for e in QUEUES] for o in ops]
+    after = [hop + (dm + o["nbytes"] / 400e3 if o["kind"] == "dma" else net if o["kind"] == "net" else 0.0) for o in ops]
+    return cost, after
 
 
 def schedule(ops, deps):
@@ -621,53 +683,7 @@ def schedule(ops, deps):
     for i in range(n):
         for j in deps[i]:
             kids[j].append(i)
-    cost = [o["cost"] for o in ops]
-    lat = [o["lat"] for o in ops]
-    engs = [o["eng"] for o in ops]
-
-    def one(pre, post, pr, back, slack):
-        left = [len(d) for d in pre]
-        ready = [lat[i] if back else 0.0 for i in range(n)]
-        pool = {}
-        for i in range(n):
-            if not left[i]:
-                pool.setdefault(engs[i], []).append(i)
-        free, order, start, fin = {}, {}, [0.0] * n, [0.0] * n
-        for _ in range(n):
-            best = None
-            for e, lst in pool.items():
-                if not lst:
-                    continue
-                t0 = max(free.get(e, 0.0), min(ready[i] for i in lst))
-                if best is None or t0 < best[0]:
-                    best = (t0, e)
-            t0, e = best
-            i = max((i for i in pool[e] if ready[i] <= t0 + slack), key=lambda i: pr[i])
-            pool[e].remove(i)
-            start[i] = max(free.get(e, 0.0), ready[i])
-            free[e] = fin[i] = start[i] + cost[i]
-            order.setdefault(e, []).append(i)
-            for k in post[i]:
-                ready[k] = max(ready[k], fin[i] + HOP + (lat[k] if back else lat[i]))
-                left[k] -= 1
-                if not left[k]:
-                    pool.setdefault(engs[k], []).append(k)
-        return order, start, fin
-    pr0 = [0.0] * n
-    for i in range(n - 1, -1, -1):
-        pr0[i] = cost[i] + lat[i] + max([pr0[k] + HOP for k in kids[i]] + [0.0])
-    best = None
-    for slack in SLACK:
-        pr = pr0
-        for _ in range(PASSES):
-            order, start, fin = one(deps, kids, pr, False, slack)
-            end = [fin[i] + lat[i] for i in range(n)]
-            if best is None or max(end) < max(best[2]):
-                best = (order, start, end, kids)
-            pr = one(kids, deps, fin, True, slack)[2]
-    seq = sorted(range(n), key=lambda i: (best[1][i], i))
-    anc = [0] * n
-    red = []
+    anc, red = [0] * n, []
     for i in range(n):
         far = 0
         for j in deps[i]:
@@ -676,54 +692,112 @@ def schedule(ops, deps):
         anc[i] = far
         for j in deps[i]:
             anc[i] |= 1 << j
+    order = red
+    pe = [o["eng"] == "tensor" for o in ops]
+    red = [[j for j in red[i] if not pe[j]] if pe[i] else red[i] for i in range(n)]
     des = [0] * n
     for i in range(n - 1, -1, -1):
         for k in kids[i]:
             des[i] |= des[k] | 1 << k
-    names = ["vector", "scalar", "tensor", "sync", "g"]
-    en = [names.index(e) for e in engs]
-    flex = [i for i in range(n) if ops[i].get("flex")]
-    after = [lat[i] + HOP for i in range(n)]
-    costs = [cost] + [[o["cost"] * (f if o.get("gather") else 1.0) * (h if o["eng"] == "tensor" else 1.0) for o in ops] for f, h in ALT]
+    tabs = [times(ops, s) for s in SPEEDS]
+    alts = [[QUEUES.index(e) for e in o["alts"]] for o in ops]
+    flex = [i for i in range(n) if len(alts[i]) > 1]
+    sinks = [i for i in range(n) if not kids[i]]
 
-    def run(seq, en, cost, why=None):
-        free = [0.0] * 5
+    cost, after = tabs[len(tabs) // 2]
+    en = [a[0] for a in alts]
+    rk = [[] for _ in range(n)]
+    for i in range(n):
+        for j in order[i]:
+            rk[j].append(i)
+
+    def listed(pre, post, pr, back):
+        left = [len(r) for r in pre]
+        ready, free, start = [after[i] if back else 0.0 for i in range(n)], [0.0] * 5, [0.0] * n
+        pool = [i for i in range(n) if not left[i]]
+        while pool:
+            t0, e = min((max(ready[i], free[en[i]]), en[i]) for i in pool)
+            i = max((i for i in pool if en[i] == e and ready[i] <= t0 + SLACK), key=lambda i: pr[i])
+            pool.remove(i)
+            start[i] = max(free[e], ready[i])
+            free[e] = start[i] + cost[i][e]
+            for k in post[i]:
+                ready[k] = max(ready[k], free[e] + (after[k] if back else after[i]))
+                left[k] -= 1
+                if not left[k]:
+                    pool.append(k)
+        return start, [start[i] + cost[i][en[i]] for i in range(n)]
+    pr = [-i for i in range(n)]
+    best = None
+    for _ in range(PASSES):
+        start, fin = listed(order, rk, pr, False)
+        if best is None or max(fin) < best[0]:
+            best = (max(fin), start)
+        pr = listed(rk, order, fin, True)[1]
+    seq = sorted(range(n), key=lambda i: (best[1][i], i))
+
+    def run(seq, en, m, fin0, q, why=None):
+        cost, after = tabs[m]
+        fin = list(fin0)
+        free = [-1.0] * 5
         who = [-1] * 5
-        fin = [0.0] * n
-        top = 0.0
-        for i in seq:
+        p, miss = q - 1, 5
+        while p >= 0 and miss:
+            i = seq[p]
             e = en[i]
-            s = free[e]
-            w = who[e]
-            for j in red[i]:
-                r = fin[j] + after[j]
-                if r > s:
-                    s = r
-                    w = j
-            s += cost[i]
-            free[e] = fin[i] = s
-            who[e] = i
-            if why is not None:
+            if free[e] < 0:
+                free[e] = fin[i] - after[i]
+                miss -= 1
+            p -= 1
+        for e in range(5):
+            if free[e] < 0:
+                free[e] = 0.0
+        if why is None:
+            for i in seq[q:]:
+                e = en[i]
+                s = free[e]
+                for j in red[i]:
+                    if fin[j] > s:
+                        s = fin[j]
+                s += cost[i][e]
+                free[e] = s
+                fin[i] = s + after[i]
+        else:
+            for i in seq:
+                e = en[i]
+                s, w = free[e], who[e]
+                for j in red[i]:
+                    if fin[j] > s:
+                        s, w = fin[j], j
+                s += cost[i][e]
+                free[e] = s
+                fin[i] = s + after[i]
+                who[e] = i
                 why[i] = w
-            if s + lat[i] > top:
-                top = s + lat[i]
-        return top, fin
-
-    def score(seq, en):
-        return sum(run(seq, en, c)[0] for c in costs) / len(costs)
+        return max(fin[i] for i in sinks), fin
     x = [SEED]
 
     def rnd(m):
         x[0] = (x[0] * 6364136223846793005 + 1442695040888963407) % 18446744073709551616
         return (x[0] >> 33) % m
-    cur = score(seq, en)
+    nm = len(tabs)
+    res = [run(seq, en, m, [0.0] * n, 0) for m in range(nm)]
+    base = [r[0] * nm for r in res]
+    fins = [r[1] for r in res]
+    mean = [[sum(tabs[m][0][i][e] / base[m] for m in range(nm)) if e in alts[i] else 0.0 for e in range(5)] for i in range(n)]
+    fixed = [sum(mean[i][e] for i in range(n) if alts[i] == [e]) for e in range(2)]
+
+    def load(en):
+        return LOAD * max(fixed[e] + sum(mean[i][e] for i in flex if en[i] == e) for e in range(2))
+    lo = load(en)
+    cur = 1.0 + lo
     top = (cur, list(seq), list(en))
-    path = []
+    path, why = [], []
     for it in range(TRIES):
         if it % 20 == 0:
             why = [-1] * n
-            fin = run(seq, en, costs[rnd(len(costs))], why)[1]
-            i = max(range(n), key=lambda i: fin[i] + lat[i])
+            fin = run(seq, en, rnd(nm), fins[0], 0, why)[1]
+            i = max(sinks, key=lambda i: fin[i])
             path = []
             while i >= 0:
                 path.append(i)
@@ -733,35 +807,46 @@ def schedule(ops, deps):
         if kind == 0:
             i = flex[rnd(len(flex))]
             en2 = list(en)
-            en2[i] = 1 - en2[i]
+            en2[i] = alts[i][(alts[i].index(en[i]) + 1 + rnd(len(alts[i]) - 1)) % len(alts[i])]
+            q = seq.index(i)
         else:
             i = path[rnd(len(path))] if kind < 7 else rnd(n)
             if kind % 2 == 0 and why[i] >= 0 and en[why[i]] == en[i]:
                 i = why[i]
             p = seq.index(i)
-            far = 1 + rnd(4) * rnd(12) + rnd(4)
+            if kind in (4, 5, 9) and len(alts[i]) > 1:
+                en2 = list(en)
+                en2[i] = alts[i][(alts[i].index(en[i]) + 1 + rnd(len(alts[i]) - 1)) % len(alts[i])]
+            far, e = 1 + rnd(2) * rnd(FAROFF), en2[i]
             if kind % 2:
-                q = max(0, p - far)
-                m = anc[i]
+                q, m = p, anc[i]
+                while q > 0 and far:
+                    q -= 1
+                    if en[seq[q]] == e and not m >> seq[q] & 1:
+                        far -= 1
+                    elif seq[q] in order[i] and en[seq[q]] == e:
+                        far -= 1
                 seq2 = seq[:q] + [j for j in seq[q:p] if m >> j & 1] + [i] + [j for j in seq[q:p] if not m >> j & 1] + seq[p + 1:]
             else:
-                q = p + 1 + far
-                m = des[i]
-                seq2 = seq[:p] + [j for j in seq[p + 1:q] if not m >> j & 1] + [i] + [j for j in seq[p + 1:q] if m >> j & 1] + seq[q:]
-            if kind == 5 and ops[i].get("flex"):
-                en2 = list(en)
-                en2[i] = 1 - en2[i]
-        v = score(seq2, en2)
+                q, r, m = p, p + 1, des[i]
+                while r < n and far:
+                    if en[seq[r]] == e:
+                        far -= 1
+                    r += 1
+                seq2 = seq[:p] + [j for j in seq[p + 1:r] if not m >> j & 1] + [i] + [j for j in seq[p + 1:r] if m >> j & 1] + seq[r:]
+            if seq2 == seq and en2 is en:
+                continue
+        res = [run(seq2, en2, m, fins[m], q) for m in range(nm)]
+        v = sum(res[m][0] / base[m] for m in range(nm)) + (load(en2) if en2 is not en else lo)
+        if en2 is not en and v <= cur + TEMP * (1.0 - it / TRIES):
+            lo2 = load(en2)
+        else:
+            lo2 = lo
         if v <= cur + TEMP * (1.0 - it / TRIES) * rnd(1000) / 1000.0:
-            cur, seq, en = v, seq2, en2
+            cur, seq, en, fins, lo = v, seq2, en2, [r[1] for r in res], lo2
             if v < top[0]:
                 top = (v, list(seq), list(en))
-    _, seq, en = top
-    fin = run(seq, en, cost)[1]
-    order = {}
-    for i in seq:
-        order.setdefault(names[en[i]], []).append(i)
-    return order, [fin[i] - cost[i] for i in range(n)], [fin[i] + lat[i] for i in range(n)], kids
+    return top[1], [QUEUES[e] for e in top[2]], kids
 
 
 PLAN = []
@@ -775,10 +860,11 @@ def rank_program(g, core, T, topo):
     deps = depends(ops)
     if not PLAN:
         PLAN.append(schedule(ops, deps))
-    order, start, end, kids = PLAN[0]
-    for e, lst in order.items():
-        for i in lst:
-            ops[i]["eng"] = e
+    seq, engs, kids = PLAN[0]
+    order = {}
+    for i in seq:
+        ops[i]["eng"] = engs[i]
+        order.setdefault(engs[i], []).append(i)
     queue = {"vector": g.vector, "scalar": g.scalar, "tensor": g.tensor, "sync": g.sync, "g": g}
     mark, total, nd, sent = {}, {}, 0, 0
     for e, lst in order.items():

from concourse.bass import DstId, RemoteDMATransfer
from concourse.mybir import dt, AluOpType, AxisListType, ActivationFunctionType

A = AluOpType
F = ActivationFunctionType
V, H, RO = 3072, 256, 3
PAD = 64
O0 = PAD + H
O1 = O0 + V
WP = O1 + H + PAD
C0, C1, CW = O0 // 16, O1 // 16, WP // 16
K = V // 16
TW = K + 16
TN = 16 * TW
FAR = 16.0
QO = 1280.0
QC, LC = 118.0, 8.0
UQ, UL, ZS = 2.0 ** -21, 2.0 ** -20, 4096.0
TOP = 3700.0
HI, LO = slice(0, 127, 18), slice(15, 114, 14)

KD = "BHF"
OPT = {
    "order": ["R2 L0 R0 R1 L1 L2"] * 3,
    "form": ["pppppp", "pppppp", "aacaac"],
    "w": ["sss", "sss", "sss"],
    "mparts": [3, 3, 3],
    "rl": ["svs", "sss", "sss"], "a1ends": [[V]] * 3,
    "a2": ["ss"] * 3, "a4": ["ss"] * 3, "a8": ["ss"] * 3, "x8": ["ss"] * 3, "xs": ["sssss"] * 3,
    "lope": (1, 0), "slots": ["QA", "QB", "QE"],
    "groups": [{("R", 2): (128, 192), ("R", 1): (0, 128), ("L", 0): (0, 64), ("L", 2): (64, 192)}] * 3,
}
SLACK, PASSES, TRIES, TEMP, SEED, LOAD, FAROFF = 0.3, 1, 120000, 0.0015, 1, 0.4, 8
SPEEDS = [(1.05, 1.15, 0.00046, 0.15, 2.0, 3.0, 1.0), (1.0, 1.56, 0.00044, 0.12, 2.2, 3.5, 1.0),
          (1.4, 1.15, 0.00062, 0.2, 2.5, 4.0, 1.2), (1.4, 1.95, 0.0006, 0.15, 2.2, 3.5, 1.0)]
CY = 0.00083

f32, b16, f16, i32, u16 = "float32", "bfloat16", "float16", "int32", "uint16"
US = ["eR", "eL", "cR", "cL", "tR", "tL", "a1", "ta", "a2", "a4", "a8", "s"]
MF = ["I", "nI", "Ih", "S1p", "S2p", "S1m", "S2m", "D1p", "D1m", "ITW", "RL", "RR", "P9", "N1"]
MB = ["I", "nI", "P9", "P9L", "P9R"]
MH = ["I", "nI", "Ih", "nTN", "n16", "P9", "N1", "P9L", "N1L", "P9R", "N1R"]

SCRATCH = {
    "XB": ("sbuf", [128, WP + O1], b16),
    "XF": ("sbuf", [128, 2 * WP + O1], f32),
    "XP": ("sbuf", [128, TN], f32), "XH": ("sbuf", [128, V], f16),
    "MA": ("sbuf", [128, O1], f32), "MB": ("sbuf", [128, O1], f32),
    "TR": ("sbuf", [128, TN], b16),
    "A2": ("sbuf", [128, O1], b16), "A4": ("sbuf", [128, O1], b16),
    "FA": ("sbuf", [128, V], f32), "FB": ("sbuf", [128, V], f32),
    "DW": ("sbuf", [128, V], f32), "MP": ("sbuf", [128, V], f32),
    "GH": ("sbuf", [128, V], f16), "PH": ("sbuf", [128, V], f16),
    "NE": ("sbuf", [128, 4096], b16),
    "VI": ("sbuf", [128, 144], b16), "VP": ("sbuf", [128, 144], f32), "PR": ("sbuf", [128, 136], b16),
    "PV": ("sbuf", [128, 2 * K], b16), "FL": ("sbuf", [128, 2 * K], b16),
    "U": ("sbuf", [128, K * len(US)], u16),
    "NR": ("sbuf", [128, 4 * CW], f32), "NL": ("sbuf", [128, 4 * CW], f32),
    "HR": ("sbuf", [128, 2 * TW], b16), "HA": ("sbuf", [128, 2 * TW], b16), "HL": ("sbuf", [128, 2 * TW], f32),
    "NA": ("sbuf", [128, K], f32), "TT": ("sbuf", [128, 2 * K], f32), "QM": ("sbuf", [128, 3 * TW], f16),
    "EN": ("sbuf", [128, K], f32), "HH": ("sbuf", [128, K], f32), "GO": ("sbuf", [128, K], f32),
    "IO": ("sbuf", [128, CW], f32), "ONF": ("sbuf", [128, 128], f32), "CB": ("sbuf", [128, 4 * K], b16),
    "LI": ("sbuf", [128, 2 * K], i32), "SI": ("sbuf", [128, 128], i32), "GI": ("sbuf", [128, 128], i32),
    "SXB": ("sbuf", [128, 512], b16), "SXF": ("sbuf", [128, 1024], f32), "SE": ("sbuf", [128, 8 * 16], f32),
    "MTF": ("sbuf", [128, 128 * len(MF)], f32), "MTB": ("sbuf", [128, 128 * len(MB)], b16),
    "MTH": ("sbuf", [128, 128 * len(MH)], f16),
    "KI": ("sbuf", [128, 8], i32), "KF": ("sbuf", [128, 16], f32), "RW": ("sbuf", [128, O0], f32),
    "QA": ("psum", [128, 1024], f32), "QB": ("psum", [128, 1024], f32),
    "QE": ("psum", [128, 1024], f32),
    "LA": ("psum", [128, 512], f32), "LB": ("psum", [128, 512], f32),
}
PSUM = ("QA", "QB", "QE", "LA", "LB")
NDMA = 100
SEMAPHORES = ["vector", "scalar", "tensor", "gcomp", "sent"] + ["arr%d" % k for k in range(14)] + ["d%d" % k for k in range(NDMA)]


def build(g, core, T, topo):
    rank = T.rank_of(core)
    n = len(T.cores)
    left, right = T.cores[(rank - 1) % n], T.cores[(rank + 1) % n]
    turn_l, turn_r = rank == 0, rank == n - 1
    ops = []
    vq, sq, pq = g.vector, g.scalar, g.tensor

    def ap(r, step=1):
        return T[r[0]][:, r[1]:r[2]:step] if step > 1 else T[r[0]][:, r[1]:r[2]]

    def sub(r, a, b):
        return (r[0], r[1] + a, r[1] + b)

    def add(alts, r, w, kind="c", cnt=1, nbytes=0):
        i = len(ops)
        o = dict(eng=list(alts)[0], alts=alts, r=list(r), w=list(w), kind=kind, cnt=cnt, nbytes=nbytes)
        o["fn"] = lambda *a: alts[o["eng"]][0](*a)
        ops.append(o)
        return i

    def two(*rs):
        return all(SCRATCH[r[0]][2] in (b16, f16, u16) for r in rs)

    def onv(fn, nel, f=1.0, kind="c"):
        return (fn, 0.06, max(64, nel * f), kind)

    def ons(fn, nel, kind="c"):
        return (fn, 0.08, max(64, nel), kind)

    def ong(fn, nel):
        return (fn, 0.17, 2 * nel, "c")

    def ts(o, i, s1, s2, o0, o1=None, extra=()):
        if o1 is None:
            fn = lambda: vq.tensor_scalar(ap(o), ap(i), s1, None, o0)
        else:
            fn = lambda: vq.tensor_scalar(ap(o), ap(i), s1, s2, o0, o1)
        return add({"vector": onv(fn, o[2] - o[1], 0.5 if two(o, i) else 1.0)}, [i] + list(extra), [o])

    def cp(o, i):
        return add({"vector": onv(lambda: vq.tensor_copy(ap(o), ap(i)), o[2] - o[1], 0.5 if two(o, i) else 1.0)}, [i], [o])

    def tt(o, a, b, op):
        f = 1.0 if a[0] in PSUM or b[0] in PSUM else 2.0
        return add({"vector": onv(lambda: vq.tensor_tensor(ap(o), ap(a), ap(b), op), o[2] - o[1], f)}, [a, b], [o])

    def act(o, i, func, scale=1.0):
        return add({"scalar": ons(lambda: sq.activation(ap(o), ap(i), func, scale=scale), o[2] - o[1])}, [i], [o])

    def ind(win, off):
        return ap(win).indirect(ap(off))

    def gat(o, win, off, first="s", scale=1.0):
        nel = o[2] - o[1]
        s = ("scalar", ons(lambda: sq.activation(ap(o), ind(win, off), F.Copy, scale=scale), nel, "g"))
        v = ("vector", onv(lambda: vq.tensor_scalar(ap(o), ind(win, off), scale, None, A.mult), nel, 1.0, "g"))
        return add(dict([s, v] if first == "s" else [v, s]), [win, off], [o])

    def gtt(o, win, off, b, op):
        return add({"vector": onv(lambda: vq.tensor_tensor(ap(o), ind(win, off), ap(b), op), o[2] - o[1], 1.0, "g")},
                   [win, off, b], [o])

    def either(o, src, scale=1.0, bias=0.0):
        nel = o[2] - o[1]
        if bias == 0.0:
            s = lambda: sq.activation(ap(o), ap(src), F.Copy, scale=scale)
            v = lambda: vq.tensor_scalar(ap(o), ap(src), scale, None, A.mult)
        else:
            s = lambda: sq.activation(ap(o), ap(src), F.Identity, bias=bias, scale=scale)
            v = lambda: vq.tensor_scalar(ap(o), ap(src), scale, bias, A.mult, A.add)
        return add({"scalar": ons(s, nel), "vector": onv(v, nel, 0.5 if two(o, src) else 1.0)}, [src], [o])

    def copy3(o, src, step=1):
        nel = o[2] - o[1]
        return add({"g": ong(lambda: g.affine_select(ap(o), ap(src, step), [[0, nel]], A.is_ge, 0.0, 0, 0), nel),
                    "scalar": ons(lambda: sq.activation(ap(o), ap(src, step), F.Copy), nel),
                    "vector": onv(lambda: vq.tensor_copy(ap(o), ap(src, step)), nel)}, [src], [o])

    def mset(o, val, step=1):
        return add({"vector": onv(lambda: vq.memset(ap(o, step), val), (o[2] - o[1]) // step, 0.5 if two(o) else 1.0)}, [], [o])

    def gc(fn, r, w, nel):
        return add({"g": ong(fn, nel)}, r, w)

    def mat(kind, name):
        k = {"F": MF, "B": MB, "H": MH}[kind].index(name)
        return ("MT" + kind, 128 * k, 128 * k + 128)

    def mm(groups, late=None, begin=True, close=True, hold=None):
        r, w, cyc = [], [hold] if hold else [], 0
        for o, terms in groups:
            w.append(o)
            for l, x, st in terms:
                r += [l, x]
                cyc += max(64, o[2] - o[1]) * (4 if SCRATCH[x[0]][2] == f32 else 1)
        if late:
            r += list(late[1][:2])

        def fn():
            last = None
            for o, terms in groups:
                if late and ops[late[0]]["eng"] == "scalar":
                    terms = terms + [late[1]]
                for k, (l, x, st) in enumerate(terms):
                    last = pq.matmul(ap(o), ap(l), ap(x, st), begin and k == 0, close and k == len(terms) - 1)
            return last
        return add({"tensor": (fn, 0.05, cyc, "p")}, r, w)

    def steps(groups, apart=False):
        nt = len(groups[0][1])
        for k in range(nt):
            for part in ([[x] for x in groups] if apart else [groups]):
                mm([(o, terms[k:k + 1]) for o, terms in part], None, k == 0, k == nt - 1)

    def tolist(o, src, more=(), late=None):
        terms = [(("VI", 16 - i, 144 - i), (src[0], src[1] + i, src[2]), 16) for i in range(16)]
        return mm([(o, terms + list(more))], late)

    def dma(q, pairs, r, w, nbytes, accum=0):
        eng = {"sync": g.sync, "scalar": g.scalar, "g": g}[q]

        def fn(sem):
            for o, i in pairs():
                if accum > 1:
                    eng.dma_start(o, i, accum_op=A.add, max_dma_last_dim=accum).then_inc(sem, 16)
                elif accum:
                    eng.dma_start(o, i, accum_op=A.add).then_inc(sem, 16)
                else:
                    eng.dma_start(o, i).then_inc(sem, 16)
        cnt = len(pairs())
        return add({q: (fn, 0.0 if q == "g" else 0.1 * cnt, cnt if q == "g" else 0, "d")}, r, w, "dma", cnt,
                   nbytes * (2 if accum else 1))

    narr = [0]

    def send(items):
        k = narr[0]
        narr[0] += 1
        per = 8 if len(items) <= 2 else 4

        def fn():
            tr = []
            for j, (dst, s, l) in enumerate(items):
                rid, pid, _ = topo.addr(dst)
                m = 0
                for e in topo.engines(core, dst)[j * per:(j + 1) * per]:
                    m |= 1 << e
                tr.append(RemoteDMATransfer(dst_ids=[DstId(rid=rid, pnc=pid)], dma_engine_mask=m,
                                            remote_sem=T.sem["arr%d" % k], src=ap(s), dst=ap(l)))
            g.remote_dma_fused(tr, local_sem=T.sem.sent)
        i = add({"g": (fn, 1.0 if k else 2.5, 0, "c")}, [s for _, s, _ in items], [l for _, _, l in items], "net", per * len(items))
        ops[i]["sem"] = "arr%d" % k
        return i

    def u(name, a=0, b=K):
        k = US.index(name) * K
        return ("U", k + a, k + b)

    def tpairs(ot, oc, it, ic, turn, way):
        def rows(t, a, b, c):
            return t[a:b, c[0]:c[1]]
        if not turn:
            return [(rows(ot, 0, 128, oc), rows(it, 0, 128, ic))]
        if way > 0:
            return [(rows(ot, 16, 128, oc), rows(it, 0, 112, ic)), (rows(ot, 0, 16, oc), rows(it, 112, 128, ic))]
        return [(rows(ot, 0, 112, oc), rows(it, 16, 128, ic)), (rows(ot, 112, 128, oc), rows(it, 0, 16, ic))]

    dma("sync", lambda: tpairs(T.SXB, (0, 256), T.x0, (0, H), turn_l, -1) + tpairs(T.SXB, (256, 512), T.x0, (V - H, V), turn_r, 1),
        [], [("SXB", 0, 512)], 128 * 1024)
    dma("scalar", lambda: tpairs(T.SI, (0, 64), T.lf, (K - 64, K), turn_r, 1) + tpairs(T.SI, (64, 128), T.rt, (K - 64, K), turn_r, 1),
        [], [("SI", 0, 128)], 128 * 512)
    dma("scalar", lambda: [(T.LI[:, 0:K], T.rt[:, :]), (T.LI[:, K:2 * K], T.lf[:, :])], [], [("LI", 0, 2 * K)], 128 * 1536)
    dma("sync", lambda: [(T.XB[:, O0:O1], T.x0[:, :])], [], [("XB", O0, O1)], 128 * 6144)
    send([(left, ("SXB", 0, 256), ("XB", O1, O1 + H)), (right, ("SXB", 256, 512), ("XB", PAD, O0)),
          (right, ("SI", 0, 128), ("GI", 0, 128))])

    def kf(j):
        return ("KF", j, j + 1)
    ONF, If = ("ONF", 0, 128), mat("F", "I")
    ONE, NEG, SEV, WPC = (("CB", j * K, j * K + K) for j in range(4))
    gc(lambda: g.iota(T.KI[:, 0:2], [[0, 2]], 0, 1), [], [("KI", 0, 2)], 2)
    mset(ONF, 1.0)
    gc(lambda: g.affine_select(ap(If), ap(ONF), [[-1, 128]], A.is_equal, 0.0, 0, 1), [ONF], [If], 128)
    gc(lambda: g.iota(T.IO[:, :], [[16, CW]], 0, 0, allow_small_or_imprecise_dtypes=True), [], [("IO", 0, CW)], CW)
    gc(lambda: g.iota(T.RW[:, :], [[1, O0]], -O0 // 2, 0, allow_small_or_imprecise_dtypes=True), [], [("RW", 0, O0)], O0)
    for c, val in ((ONE, 1.0), (NEG, -1.0), (SEV, 7.0), (WPC, float(WP))):
        mset(c, val)
    ts(("KI", 2, 3), ("KI", 0, 1), 15, None, A.bitwise_and)
    ts(("KI", 3, 4), ("KI", 0, 1), 1, None, A.bitwise_and)
    cp(("KF", 0, 2), ("KI", 2, 4))
    ts(kf(2), kf(0), 0.0, None, A.is_equal)
    ts(kf(3), kf(0), 1.0, float(O0 // 2), A.is_equal, A.mult)
    ts(kf(4), kf(1), -1.0, UQ * ZS, A.add, A.mult)
    ts(kf(5), kf(1), -UL * ZS, None, A.mult)
    ts(kf(6), kf(0), -LC - 1.0, ap(kf(5)), A.add, A.mult, extra=[kf(5)])
    ts(kf(7), kf(0), -LC, ap(kf(5)), A.add, A.mult, extra=[kf(5)])
    for j in range(2):
        r0 = O0 // 2 + C0 - int(QC)
        ts(("PV", j * K, j * K + K), ("RW", r0, r0 + K), ap(kf(4)), ap(kf(6 + j)), A.mult, A.add, extra=[kf(4), kf(6 + j)])
    ts(("IO", 0, CW), ("IO", 0, CW), ap(kf(0)), None, A.add, extra=[kf(0)])
    for b, o in (("XB", 0), ("XF", 0), ("XF", WP)):
        mset((b, o, o + PAD), FAR)
        mset((b, o + WP - PAD, o + WP), FAR)

    def scaled(o, c, turn=False, way=0):
        if not way:
            either(o, If, c)
            return
        a, b = (16, 112) if way > 0 else (112, 16)
        either(sub(o, a, 128), sub(If, 0, b) if turn else sub(If, a, 128), c)
        either(sub(o, 0, a), sub(If, b, 128) if turn else sub(If, 0, a), c)

    def strided(o, o0, i0):
        return add({"vector": onv(lambda: vq.tensor_copy(ap(sub(o, o0, 128), 16), ap(sub(If, i0, 128), 16)), 8)}, [If], [o])
    for s1, s2, d1, a, b in (("S1p", "S2p", "D1p", 1, 0), ("S1m", "S2m", "D1m", 0, 1)):
        m = mat("F", s1)
        cp(sub(m, a, 128 - b), sub(If, b, 128 - a))
        mset(sub(m, 15 * b, 128), 0.0, 16)
        tt(mat("F", d1), m, If, A.subtract)
        m = mat("F", s2)
        mset(m, 0.0)
        strided(m, 15 * b, 15 * a)
    mset(("VI", 0, 144), 0.0)
    gc(lambda: g.affine_select(T.VI[:, 16:144:16], T.ONF[:, 0:8], [[-16, 8]], A.is_ge, 0.0, 0, 1), [ONF], [("VI", 0, 144)], 8)
    gc(lambda: g.affine_select(T.VI[:, 16:144:16], T.VI[:, 16:144:16], [[16, 8]], A.is_ge, 0.0, 15, -1), [], [("VI", 0, 144)], 8)
    mset(("VP", 0, 144), 0.0)
    mset(("KF", 8, 16), ZS)
    for j, s in enumerate((HI, LO)):
        gc(lambda j=j, s=s: g.affine_select(T.VP[:, 16 + j:144:16], T.KF[:, 8:16], [[-s.step, 8]], A.is_equal, 0.0, -s.start, 1),
           [("KF", 8, 16)], [("VP", 0, 144)], 8)
    mset(("PR", 0, 136), 0.0)
    add({"vector": onv(lambda: vq.tensor_tensor(T.PR[:, 1:129:2], ap(If, 2), ap(sub(If, 1, 128), 2), A.add), 64, 2.0)},
        [If], [("PR", 0, 136)])
    either(("PR", 0, 136), ("PR", 0, 136), 8192.0)
    for kd, nm, c in (("H", "I", 1.0), ("H", "Ih", 0.5), ("B", "I", 1.0), ("B", "nI", -1.0), ("F", "ITW", float(TW)),
                      ("H", "nTN", -float(TN)), ("H", "n16", -16.0), ("H", "N1", -0.125), ("B", "P9", 1.125),
                      ("H", "nI", -1.0), ("H", "P9", 1.125), ("F", "nI", -1.0), ("F", "Ih", 0.5), ("F", "P9", 1.125),
                      ("F", "N1", -0.125)):
        if nm != "Ih" or kd != "F" or "p" in OPT["form"][2]:
            scaled(mat(kd, nm), c)
    for kd, nm, c in (("F", "R", 1.0), ("B", "P9", 1.125), ("H", "P9", 1.125), ("H", "N1", -0.125)):
        scaled(mat(kd, nm + "L"), c, turn_l, -1)
        scaled(mat(kd, nm + "R"), c, turn_r, 1)
    for a in range(0, TN, TN // 4):
        add({"g": ong(lambda a=a: g.iota(T.TR[:, a:a + TN // 4], [[0, TN // 4]], 0, 0, allow_small_or_imprecise_dtypes=True), TN // 4),
             "vector": onv(lambda a=a: vq.memset(T.TR[:, a:a + TN // 4], 0.0), TN // 4, 0.5)}, [], [("TR", a, a + TN // 4)])
    for b in ("A2", "A4"):
        ts((b, 0, O0), ("RW", 0, O0), ap(kf(2)), ap(kf(3)), A.mult, A.add, extra=[("KF", 2, 4)])
    cp(("HA", 0, 16), ("IO", C0 - 16, C0))
    tt(("HA", TW, TW + 16), ("IO", C0 - 16, C0), ("HA", 0, 16), A.subtract)
    IOo = ("IO", C0, C1)

    def nl(k, t, a, b):
        return ("N" + k, t * CW + a, t * CW + b)

    for j, k in enumerate("RL"):
        ts(nl(k, 0, C0, C1), ("LI", j * K, j * K + K), float(PAD), None, A.add)
        ts(u("e" + k), ("LI", j * K, j * K + K), float(PAD), None, A.add)
    ts(nl("L", 0, C0 - 1, C0), ("GI", 63, 64), float(PAD - V), None, A.add)
    ts(nl("R", 0, C0 - 1, C0), ("GI", 127, 128), float(PAD - V), None, A.add)

    bank = {"R": "LA", "L": "LB"}

    def cands(t):
        d = 1 if t % 2 == 0 else -1
        sfx = "p" if d > 0 else "m"
        for k in "RL":
            far = (mat("F", "S2" + sfx), nl(k, t, C0 - d, C1 - d), 1)
            mm([((bank[k], 0, K), [(mat("F", "S1" + sfx), nl(k, t, C0, C1), 1), far])])
            if k == "R":
                ts(u("cR"), (bank[k], 0, K), float(d), float(WP - PAD), A.add, A.min)
            else:
                ts(u("cL"), (bank[k], 0, K), float(d), float(PAD - 1), A.add, A.max)
            mm([((bank[k], K, 2 * K), [(mat("F", "D1" + sfx), nl(k, t, C0, C1), 1), far, (mat("B", "I"), ONE if d > 0 else NEG, 1)])])

    def table(h):
        dma("sync", lambda: [(T.TR[HI, :], T[h][:, 0:TW]), (T.TR[LO, :], T[h][:, TW:2 * TW])], [(h, 0, 2 * TW)], [("TR", 0, TN)], 128 * 1000)

    def quot(qm, src):
        either(qm, src, 0.0625, QO - 0.46875)

    def tabpos(o, src, qm, ps, first):
        quot(qm, src)
        mm([(ps, [(mat("F", "ITW"), src, 1), (mat("H", "nTN"), qm, 1), (mat("H", "I"), qm, 1)])])
        ts(o, ps, (TN - 1) * QO - first, None, A.add)

    def hilo(h, src, a, b, ps=None):
        either((h, a, b), src)
        if ps:
            ps = (ps[0], ps[1], ps[1] + b - a)
            mm([(ps, [(If, src, 1), (mat("B", "nI"), (h, a, b), 1)])])
            either((h, TW + a, TW + b), ps)
        else:
            tt((h, TW + a, TW + b), src, (h, a, b), A.subtract)

    nse = [0]

    def edges(t, what, bk):
        gr, items = [], []
        for m, (k, way) in enumerate(what):
            ps, se = (bk, 384 + 16 * m, 400 + 16 * m), ("SE", nse[0], nse[0] + 16)
            nse[0] += 16
            if way < 0:
                gr.append((ps, [(mat("F", "RL"), nl(k, t + 1, C0, C0 + 16), 1)]))
                items.append((left, se, nl(k, t + 1, C1, C1 + 16)))
            else:
                gr.append((ps, [(mat("F", "RR"), nl(k, t + 1, C1 - 16, C1), 1)]))
                items.append((right, se, nl(k, t + 1, C0 - 16, C0)))
        mm(gr)
        for (ps, _), (k, way), it in zip(gr, what, items):
            if (k, way) == ("L", -1):
                ts(it[1], ps, float(V), TOP, A.add, A.min)
            else:
                either(it[1], ps, 1.0, -float(way * V))
        send(items)

    qn = [0]

    def qslot():
        qn[0] += 1
        return "QA" if qn[0] % 2 else "QB"
    en = [0]

    def eslot():
        en[0] += 1
        return 512 * (en[0] % 2)

    XS = [("XB", 0), ("XF", WP), ("XF", 0)]
    cands(0)
    pend = []
    for t in range(RO):
        xb, xo = XS[t]
        kd = KD[t]
        kg = "F" if kd == "F" else "H"
        win = (xb, xo, xo + WP)
        last = t == RO - 1
        order = [(x[0], int(x[1])) for x in OPT["order"][t].split()]

        def xown(a, b):
            return (xb, xo + O0 + a, xo + O0 + b)

        def xpe(a, b):
            return ("XH", a, b) if kd == "H" else xown(a, b)

        def xc(a, b):
            return ("XH", a, b) if kd == "H" else (xb, xo + WP + O0 + a, xo + WP + O0 + b)

        def ge(a, b):
            return ("FA" if kd == "F" else "GH", a, b)

        def pp(a, b):
            return ("FB" if kd == "F" else "PH", a, b)
        for c in (2, 0, 1):
            a, b = 1024 * c, 1024 * c + 1024
            if kd == "H":
                copy3(xc(a, a + 512), xown(a, a + 512))
                copy3(xc(a + 512, b), xown(a + 512, b))
            elif t:
                dma("sync", lambda o=xc(a, b), i=xown(a, b): [(ap(o), ap(i))], [xown(a, b)], [xc(a, b)], 512 * 1024)
        if t == 0:
            dma("sync", lambda o=xc(0, V): [(ap(o), T.x0[:, :])], [], [xc(0, V)], 128 * 6144)
        dma("sync", lambda xb=xb, xo=xo: [(T[xb][:, xo + WP:xo + WP + O0], T[xb][:, xo:xo + O0])],
            [(xb, xo, xo + O0)], [(xb, xo + WP, xo + WP + O0)], 128 * 1280)
        for i in range(16):
            copy3(("XP", TW * i, TW * i + TW), (xb, xo + O0 + i, xo + O1 + H), 16)
        main = {"R": ("R", 1), "L": ("L", -1)}
        extra = [] if last else [("L", 1)] if t % 2 else [("R", -1)]
        done = []
        for nc, (k, c) in enumerate(order):
            bk = bank[k]
            j = "RL".index(k)
            jq = j * TW
            if True:
                a, b = 1024 * c, 1024 * c + 1024
                ue, uc = u("e" + k, 64 * c, 64 * c + 64), u("c" + k, 64 * c, 64 * c + 64)
                q = OPT["slots"][nc % len(OPT["slots"])]
                form = OPT["form"][t][nc]
                r0 = 1024 * (nc % 3)
                g1, p1 = ge(r0, r0 + 1024), pp(r0, r0 + 1024)
                ne = ("NE", 1024 * (nc % 4), 1024 * (nc % 4) + 1024)
                late = None
                if form == "a":
                    gtt(g1, win, uc, xc(a, b), A.subtract)
                    gtt(p1, win, ue, xc(a, b), A.subtract)
                    act((q, 0, 1024), g1, F.Abs)
                    act(p1, p1, F.Abs)
                    tt(ne, (q, 0, 1024), p1, A.is_lt)
                elif form == "c":
                    gat(g1, win, uc)
                    gtt(p1, win, ue, xc(a, b), A.subtract)
                    steps([((q, s, s + 512), [(mat(kd, "nI"), xpe(a + s, a + s + 512), 1), (mat(kg, "I"), sub(g1, s, s + 512), 1)]) for s in (0, 512)], True)
                    act((q, 0, 1024), (q, 0, 1024), F.Abs)
                    act(p1, p1, F.Abs)
                    tt(ne, (q, 0, 1024), p1, A.is_lt)
                else:
                    gat(g1, win, ue)
                    gtt(p1, win, uc, g1, A.subtract)
                    steps([((q, s, s + 512), [(mat(kd, "nI"), xpe(a + s, a + s + 512), 1), (mat(kg, "I"), sub(g1, s, s + 512), 1),
                                              (mat(kg, "Ih"), sub(p1, s, s + 512), 1)]) for s in (0, 512)], kd == "F")
                    tt(ne, (q, 0, 1024), p1, A.mult)
                    i = add({"scalar": ons(lambda ne=ne: sq.activation(ap(ne), ap(ne), F.Sign, bias=-2.0 ** -27, scale=-1.0), 1024),
                             "vector": onv(lambda ne=ne: vq.tensor_scalar(ap(ne), ap(ne), 0.0, None, A.is_lt), 1024, 0.5)}, [ne], [ne])
                    late = (i, (mat("B", "I"), sub(SEV, 0, 64), 1))
                tolist((bk, 64 * c, 64 * c + 64), ne, late=late)
                if (k, c) not in OPT["groups"][t]:
                    continue
                ca, cb = OPT["groups"][t][k, c]
                tv = ("TT", j * K + ca, j * K + cb)
                new = nl(k, t + 1, C0 + ca, C0 + cb)
                ts(tv, (bk, ca, cb), 8.5, None, A.is_ge)
                tt((bk, K + ca, K + cb), (bk, K + ca, K + cb), tv, A.mult)
                tt(new, (bk, K + ca, K + cb), nl(k, t, C0 + ca, C0 + cb), A.add)
                done += [(k, -1)] * (ca == 0) + [(k, 1)] * (cb == K)
                if main.get(k) in done:
                    now = [main.pop(k)] + [e for e in extra if e in done]
                    extra = [e for e in extra if e not in now]
                    edges(t, now, bk)
                tabpos(u("t" + k, ca, cb), new, ("QM", jq + ca, jq + cb), (bk, ca, cb), C0 if k == "R" else C0 - 16)
            if k in [x[0] for x in order[nc + 1:]]:
                continue
            if not last:
                pend.append(lambda k=k, t=t: cp(u("e" + k), nl(k, t + 1, C0, C1)))
            if k == "R":
                hilo("HR", nl(k, t + 1, C0 - 16, C1), 0, TW, (bk, 0) if OPT["lope"][0] else None)
                table("HR")
            else:
                qm = ("QM", jq, jq + TW)
                quot(sub(qm, K, TW), nl(k, t + 1, C1, C1 + 16))
                either(("HL", 0, TW), qm, UQ, -(QO + QC) * UQ)
                mm([((bk, 0, TW), [(If, nl(k, t + 1, C0, C1 + 16), 1), (mat("H", "n16"), qm, 1)])])
                either(("HL", TW, 2 * TW), (bk, 0, TW), UL, (16 * QO - LC) * UL)
                for j, s in enumerate((HI, LO)):
                    i = dma("g", lambda j=j, s=s: [(T.XP[s, :], T.HL[:, j * TW:j * TW + TW])],
                            [("HL", j * TW, j * TW + TW)], [("XP", 0, TN)], 128 * 1000, accum=4 * TW)
                    ops[i]["beside"] = t
        if extra:
            edges(t, extra, bank[extra[0][0]])
        def cut(name):
            e = OPT[name][t]
            return [(V // len(e) * h, V // len(e) * (h + 1), e[h]) for h in range(len(e))]

        def mstep(src, lst, first, nxt, t=t, xc=xc):
            w = V // OPT["mparts"][t]
            for a in range(0, V, w):
                b = a + w
                gtt(("MP", a, b), (src[0], src[1], src[1] + O0 + b), u(lst, a // 16, b // 16), xc(a, b) if first else ("MP", a, b), A.max)
                if nxt:
                    dma("sync", lambda a=a, b=b: [(T[nxt][:, O0 + a:O0 + b], T.MP[:, a:b])], [("MP", a, b)], [(nxt, O0 + a, O0 + b)], 512 * (b - a))
        for a, b, e in cut("rl"):
            gat(("A4", O0 + a, O0 + b), ("TR", 0, TN), u("tL", a // 16, b // 16), e)
            tolist(("LA", a // 16, b // 16), ("A4", O0 + a, O0 + b))
            if b in OPT["a1ends"][t]:
                ca, cb = ([0] + [x // 16 for x in OPT["a1ends"][t] if x < b])[-1], b // 16
                ps, io, na = ("LA", ca, cb), ("IO", C0 + ca, C0 + cb), ("NA", ca, cb)
                tt(ps, ps, io, A.not_equal)
                tt(ps, ps, io, A.mult)
                tt(na, ps, nl("L", t + 1, C0 + ca, C0 + cb), A.max)
                hilo("HA", na, 16 + ca, 16 + cb, ("LA", ca) if OPT["lope"][1] else None)
                if b == V:
                    table("HA")
                cp(u("a1", ca, cb), na)
                tabpos(u("ta", ca, cb), na, ("QM", 2 * TW + ca, 2 * TW + cb), ps, C0 - 16)
        for fn in pend:
            fn()
        dma("g" if xb == "XB" else "sync",
            lambda xb=xb, xo=xo: [(T.MA[:, 0:O0], T[xb][:, xo:xo + O0]), (T.MB[:, 0:O0], T[xb][:, xo:xo + O0])],
            [(xb, xo, xo + O0)], [("MA", 0, O0), ("MB", 0, O0)], 128 * 2560)
        mstep((xb, xo), "a1", True, "MA")
        nb = [0]

        def lists(name, o, src, lst, more=None):
            for a, b, e in cut(name):
                ca, cb = a // 16, b // 16
                nb[0] += 1
                ps = ("LA" if nb[0] % 2 else "LB", 0, cb - ca)
                gat((o, O0 + a, O0 + b), (src, 0, TN if src == "TR" else O0 + b), u(lst, ca, cb), e)
                tolist(ps, (o, O0 + a, O0 + b), [(mat("B", "I"), sub(more, 0, cb - ca), 1)] if more else [])
                yield ca, cb, ps
        for ca, cb, ps in lists("a2", "A2", "TR", "ta"):
            cp(u("a2", ca, cb), ps)
            either(("HH", ca, cb), ps)
        zb = "QE"
        pend = []
        for c in range(3):
            a, b = 1024 * c, 1024 * c + 1024
            ut = u("tR", 64 * c, 64 * c + 64)
            fused = OPT["w"][t][c] == "v"
            if fused:
                gtt(("DW", a, b), ("XP", 0, TN), ut, xown(a, b), A.subtract)
            else:
                gat(("DW", a, b), ("XP", 0, TN), ut, "s", -1.0)
            for j in range(2):
                zo = (zb, j * K + 64 * c, j * K + 64 * c + 64)
                terms = [(("VP", 16 - r, 144 - r), ("DW", a + r + j, b), 16) for r in range(0, 16, 2)]
                terms.append((mat("B", "I" if fused else "nI"), ("PV", j * K + 64 * c, j * K + 64 * c + 64), 1))
                mm([(zo, terms[:4])], None, True, False, (zb, 0, 512))
                mm([(zo, terms[4:])], None, False, True, (zb, 0, 512))
            if not fused:
                dma("g", lambda a=a, b=b, i=xown(a, b): [(T.DW[:, a:b], ap(i))], [xown(a, b)], [("DW", a, b)], 512 * 1024, accum=1)
            pend.append(lambda a=a, b=b: act(("DW", a, b), ("DW", a, b), F.Abs))
        mstep(("MA", 0), "a2", False, "MB")
        for ca, cb, ps in lists("a4", "A4", "A2", "a2"):
            cp(u("a4", ca, cb), ps)
            tt(("GO", ca, cb), ps, ("HH", ca, cb), A.is_lt)
        cp(("LI", 0, 2 * K), (zb, 0, 2 * K))
        tt(("FL", 0, 2 * K), (zb, 0, 2 * K), ("LI", 0, 2 * K), A.not_equal)
        mm([((zb, 0, K), [(("PR", 1, 129), ("FL", 0, K), 1), (("PR", 0, 128), ("FL", K, 2 * K), 1)])])
        tt((zb, 0, K), (zb, 0, K), ("GO", 0, K), A.mult)
        tt(("GO", 0, K), (zb, 0, K), IOo, A.max)
        for ca, cb, ps in lists("a8", "A2", "A4", "a4", WPC):
            ts(u("a8", ca, cb), ps, -float(WP), None, A.add)
            tt(ps, ps, ("GO", ca, cb), A.min)
            cp(u("s", ca, cb), ps)
        mstep(("MB", 0), "a4", False, "MA")
        if not last:
            cands(t + 1)
        for a, b, e in cut("x8"):
            gat((xb, xo + WP + O0 + a, xo + WP + O0 + b), (xb, xo, xo + O0 + b), u("a8", a // 16, b // 16), e)
        nxs = [0]

        def xs(a, b):
            gat(ge(a, b), (xb, xo, xo + WP + O0 + b), u("s", a // 16, b // 16), OPT["xs"][t][nxs[0]])
            nxs[0] += 1

        def zz(o, a, b, sfx):
            return (o, [(mat(kd, "P9" + sfx), xpe(a, b), 1), (mat(kg, "N1" + sfx), ge(a, b), 1)])
        if not last:
            nb, no = XS[t + 1]
            xs(0, H)
            xs(V - H, V)
            q = qslot()
            mm([zz((q, 0, H), 0, H, "L"), zz((q, H, 2 * H), V - H, V, "R")])
            sx = 512 * t
            ts(("SXF", sx, sx + 512), (q, 0, 512), 0.0, 4.0, A.max, A.min)
            send([(left, ("SXF", sx, sx + H), (nb, no + O1, no + O1 + H)), (right, ("SXF", sx + H, sx + 512), (nb, no + PAD, no + O0))])
            for a, b in ((H, 1024), (1024, 2048), (2048, V - H)):
                xs(a, b)
            for a in (2048, 0, 1024):
                q = qslot()
                steps([zz((q, s - a, s - a + 512), s, s + 512, "") for s in (a, a + 512)])
                ts((nb, no + O0 + a, no + O0 + a + 1024), (q, 0, 1024), 0.0, 4.0, A.max, A.min)
        else:
            for a, b, q in ((0, 1024, "QA"), (1024, 2048, "QB"), (2048, 2560, "LA"), (2560, V, "LB")):
                two_terms = [zz((q, s - a, s - a + 512), s, s + 512, "") for s in range(a, b, 512)]
                for o, terms in two_terms:
                    mm([(o, terms[:1])], close=False)
                xs(a, b)
                for o, terms in two_terms:
                    mm([(o, terms[1:])], begin=False)
                ts(pp(a, b), (q, 0, b - a), 0.0, 4.0, A.max, A.min)
                dma("sync", lambda a=a, b=b, i=pp(a, b): [(T.xe[:, a:b], ap(i))], [pp(a, b)], [], 512 * (b - a))
        def grow(t=t, last=last, mstep=mstep):
            mstep(("MA", 0), "a8", False, None)
            w = 512 if last else 1024
            ends = [1024, 2048, 2560, V] if last else [2048, V]
            s0 = 0
            for s in range(0, V, w):
                e = sub(("QE", eslot(), 0), 0, w) if last else (qslot(), 0, w)
                act(e, ("DW", s, s + w), F.Exp, scale=-1.0)
                yb = "DW" if last else "FB"
                tt((yb, s, s + w), e, ("MP", s, s + w), A.mult)
                if s + w in ends:
                    dma("g" if t else "sync", lambda a=s0, b=s + w, yb=yb: [(T.ye[:, a:b], T[yb][:, a:b])], [(yb, s0, s + w)],
                        [("ye", s0, s + w)], 512 * (s + w - s0), accum=int(t > 0))
                    s0 = s + w
        pend.append(grow)
    for fn in pend:
        fn()
    return ops


def depends(ops):
    seen = {}
    deps = []
    for i, o in enumerate(ops):
        d = set()
        acc = [(r, False) for r in o["r"]] + [(w, True) for w in o["w"]]
        for (nm, a, b), wr in acc:
            for j, a2, b2, wr2 in seen.get(nm, ()):
                if nm in PSUM and (ops[j]["eng"] != o["eng"] or len(o["alts"]) > 1 or len(ops[j]["alts"]) > 1):
                    if a // 512 <= (b2 - 1) // 512 and a2 // 512 <= (b - 1) // 512:
                        d.add(j)
                elif (wr or wr2) and a < b2 and a2 < b and o.get("beside", -1) != ops[j].get("beside", -2):
                    d.add(j)
        for (nm, a, b), wr in acc:
            seen.setdefault(nm, []).append((i, a, b, wr))
        d.discard(i)
        deps.append(d)
    return deps


QUEUES = ["vector", "scalar", "tensor", "sync", "g"]


def times(ops, speed):
    f, ga, pe, hop, dm, net, gd = speed
    per = {"c": CY * f, "g": CY * f * ga, "p": pe, "d": gd}
    cost = [[o["alts"][e][1] + o["alts"][e][2] * per[o["alts"][e][3]] if e in o["alts"] else None for e in QUEUES] for o in ops]
    after = [hop + (dm + o["nbytes"] / 400e3 if o["kind"] == "dma" else net if o["kind"] == "net" else 0.0) for o in ops]
    return cost, after


def schedule(ops, deps):
    n = len(ops)
    kids = [[] for _ in range(n)]
    for i in range(n):
        for j in deps[i]:
            kids[j].append(i)
    anc, red = [0] * n, []
    for i in range(n):
        far = 0
        for j in deps[i]:
            far |= anc[j]
        red.append([j for j in deps[i] if not far >> j & 1])
        anc[i] = far
        for j in deps[i]:
            anc[i] |= 1 << j
    order = red
    pe = [o["eng"] == "tensor" for o in ops]
    red = [[j for j in red[i] if not pe[j]] if pe[i] else red[i] for i in range(n)]
    des = [0] * n
    for i in range(n - 1, -1, -1):
        for k in kids[i]:
            des[i] |= des[k] | 1 << k
    tabs = [times(ops, s) for s in SPEEDS]
    alts = [[QUEUES.index(e) for e in o["alts"]] for o in ops]
    flex = [i for i in range(n) if len(alts[i]) > 1]
    sinks = [i for i in range(n) if not kids[i]]

    cost, after = tabs[len(tabs) // 2]
    en = [a[0] for a in alts]
    rk = [[] for _ in range(n)]
    for i in range(n):
        for j in order[i]:
            rk[j].append(i)

    def listed(pre, post, pr, back):
        left = [len(r) for r in pre]
        ready, free, start = [after[i] if back else 0.0 for i in range(n)], [0.0] * 5, [0.0] * n
        pool = [i for i in range(n) if not left[i]]
        while pool:
            t0, e = min((max(ready[i], free[en[i]]), en[i]) for i in pool)
            i = max((i for i in pool if en[i] == e and ready[i] <= t0 + SLACK), key=lambda i: pr[i])
            pool.remove(i)
            start[i] = max(free[e], ready[i])
            free[e] = start[i] + cost[i][e]
            for k in post[i]:
                ready[k] = max(ready[k], free[e] + (after[k] if back else after[i]))
                left[k] -= 1
                if not left[k]:
                    pool.append(k)
        return start, [start[i] + cost[i][en[i]] for i in range(n)]
    pr = [-i for i in range(n)]
    best = None
    for _ in range(PASSES):
        start, fin = listed(order, rk, pr, False)
        if best is None or max(fin) < best[0]:
            best = (max(fin), start)
        pr = listed(rk, order, fin, True)[1]
    seq = sorted(range(n), key=lambda i: (best[1][i], i))

    def run(seq, en, m, fin0, q, why=None):
        cost, after = tabs[m]
        fin = list(fin0)
        free = [-1.0] * 5
        who = [-1] * 5
        p, miss = q - 1, 5
        while p >= 0 and miss:
            i = seq[p]
            e = en[i]
            if free[e] < 0:
                free[e] = fin[i] - after[i]
                miss -= 1
            p -= 1
        for e in range(5):
            if free[e] < 0:
                free[e] = 0.0
        if why is None:
            for i in seq[q:]:
                e = en[i]
                s = free[e]
                for j in red[i]:
                    if fin[j] > s:
                        s = fin[j]
                s += cost[i][e]
                free[e] = s
                fin[i] = s + after[i]
        else:
            for i in seq:
                e = en[i]
                s, w = free[e], who[e]
                for j in red[i]:
                    if fin[j] > s:
                        s, w = fin[j], j
                s += cost[i][e]
                free[e] = s
                fin[i] = s + after[i]
                who[e] = i
                why[i] = w
        return max(fin[i] for i in sinks), fin
    x = [SEED]

    def rnd(m):
        x[0] = (x[0] * 6364136223846793005 + 1442695040888963407) % 18446744073709551616
        return (x[0] >> 33) % m
    nm = len(tabs)
    res = [run(seq, en, m, [0.0] * n, 0) for m in range(nm)]
    base = [r[0] * nm for r in res]
    fins = [r[1] for r in res]
    mean = [[sum(tabs[m][0][i][e] / base[m] for m in range(nm)) if e in alts[i] else 0.0 for e in range(5)] for i in range(n)]
    fixed = [sum(mean[i][e] for i in range(n) if alts[i] == [e]) for e in range(2)]

    def load(en):
        return LOAD * max(fixed[e] + sum(mean[i][e] for i in flex if en[i] == e) for e in range(2))
    lo = load(en)
    cur = 1.0 + lo
    top = (cur, list(seq), list(en))
    path, why = [], []
    for it in range(TRIES):
        if it % 20 == 0:
            why = [-1] * n
            fin = run(seq, en, rnd(nm), fins[0], 0, why)[1]
            i = max(sinks, key=lambda i: fin[i])
            path = []
            while i >= 0:
                path.append(i)
                i = why[i]
        kind = rnd(10)
        en2, seq2 = en, seq
        if kind == 0:
            i = flex[rnd(len(flex))]
            en2 = list(en)
            en2[i] = alts[i][(alts[i].index(en[i]) + 1 + rnd(len(alts[i]) - 1)) % len(alts[i])]
            q = seq.index(i)
        else:
            i = path[rnd(len(path))] if kind < 7 else rnd(n)
            if kind % 2 == 0 and why[i] >= 0 and en[why[i]] == en[i]:
                i = why[i]
            p = seq.index(i)
            if kind in (4, 5, 9) and len(alts[i]) > 1:
                en2 = list(en)
                en2[i] = alts[i][(alts[i].index(en[i]) + 1 + rnd(len(alts[i]) - 1)) % len(alts[i])]
            far, e = 1 + rnd(2) * rnd(FAROFF), en2[i]
            if kind % 2:
                q, m = p, anc[i]
                while q > 0 and far:
                    q -= 1
                    if en[seq[q]] == e and not m >> seq[q] & 1:
                        far -= 1
                    elif seq[q] in order[i] and en[seq[q]] == e:
                        far -= 1
                seq2 = seq[:q] + [j for j in seq[q:p] if m >> j & 1] + [i] + [j for j in seq[q:p] if not m >> j & 1] + seq[p + 1:]
            else:
                q, r, m = p, p + 1, des[i]
                while r < n and far:
                    if en[seq[r]] == e:
                        far -= 1
                    r += 1
                seq2 = seq[:p] + [j for j in seq[p + 1:r] if not m >> j & 1] + [i] + [j for j in seq[p + 1:r] if m >> j & 1] + seq[r:]
            if seq2 == seq and en2 is en:
                continue
        res = [run(seq2, en2, m, fins[m], q) for m in range(nm)]
        v = sum(res[m][0] / base[m] for m in range(nm)) + (load(en2) if en2 is not en else lo)
        if en2 is not en and v <= cur + TEMP * (1.0 - it / TRIES):
            lo2 = load(en2)
        else:
            lo2 = lo
        if v <= cur + TEMP * (1.0 - it / TRIES) * rnd(1000) / 1000.0:
            cur, seq, en, fins, lo = v, seq2, en2, [r[1] for r in res], lo2
            if v < top[0]:
                top = (v, list(seq), list(en))
    return top[1], [QUEUES[e] for e in top[2]], kids


PLAN = []


def rank_program(g, core, T, topo):
    rank = T.rank_of(core)
    if rank is None:
        return
    ops = build(g, core, T, topo)
    deps = depends(ops)
    if not PLAN:
        PLAN.append(schedule(ops, deps))
    seq, engs, kids = PLAN[0]
    order = {}
    for i in seq:
        ops[i]["eng"] = engs[i]
        order.setdefault(engs[i], []).append(i)
    queue = {"vector": g.vector, "scalar": g.scalar, "tensor": g.tensor, "sync": g.sync, "g": g}
    mark, total, nd, sent = {}, {}, 0, 0
    for e, lst in order.items():
        for i in lst:
            o = ops[i]
            if o["kind"] == "dma":
                mark[i] = ("d%d" % nd, 16 * o["cnt"])
                nd += 1
            elif o["kind"] == "net":
                mark[i] = (o["sem"], o["cnt"])
                sent += o["cnt"]
            elif kids[i]:
                s = "gcomp" if e == "g" else e
                mark[i] = (s, total.get(s, 0) + 1)
            if i in mark:
                total[mark[i][0]] = mark[i][1]
    for e, lst in order.items():
        q, seen = queue[e], {}
        for i in lst:
            o = ops[i]
            need = {}
            for j in deps[i]:
                if e == "tensor" and ops[j]["eng"] == "tensor":
                    continue
                s, c = mark[j]
                if c > seen.get(s, 0) and c > need.get(s, 0):
                    need[s] = c
            for s, c in need.items():
                q.wait_ge(T.sem[s], c)
                seen[s] = c
            if o["kind"] == "dma":
                o["fn"](T.sem[mark[i][0]])
            elif o["kind"] == "net":
                o["fn"]()
            else:
                ins = o["fn"]()
                if i in mark:
                    ins.then_inc(T.sem[mark[i][0]], 1)
    for s, c in total.items():
        g.wait_ge(T.sem[s], c)
    g.wait_ge(T.sem.sent, sent)
